import numpy as np
import ml_dtypes


def mxq(x, axis, fmt="e4m3"):
    dtype, down = {"e4m3": (ml_dtypes.float8_e4m3fn, 7), "e5m2": (ml_dtypes.float8_e5m2, 14)}[fmt]
    v = np.moveaxis(np.asarray(x, np.float32).astype(ml_dtypes.bfloat16).astype(np.float64), axis, -1)
    blocks = v.reshape(v.shape[:-1] + (-1, 32))
    amax = np.abs(blocks).max(-1, keepdims=True)
    byte = np.maximum(np.where(amax > 0, np.frexp(amax)[1] - 1 + 127, 0) - down, 1)
    scale = np.exp2(byte - 127.0)
    codes = (blocks / scale).astype(np.float32).astype(dtype).astype(np.float64)
    return np.moveaxis((codes * scale).reshape(v.shape), -1, axis)


WIDE = False


def mx_kscale(k):
    if not WIDE:
        return np.ones(k)
    levels = np.array([10, -10, 5, -5, 0])
    if k % 512:
        return np.exp2(np.random.permutation(np.resize(levels, k // 32))).repeat(32)
    a = np.empty((k // 512, 16))
    for p in range(k // 512):
        a[p, :8] = np.random.permutation(np.resize(levels, 8))
        for g in range(8):
            far = levels[np.abs(levels - a[p, g]) >= 10]
            a[p, g + 8] = far[np.random.randint(len(far))]
    return np.exp2(a.ravel()).repeat(32)


BF16 = ml_dtypes.bfloat16


def bf(x):
    return np.asarray(x, np.float32).astype(BF16)


def f64(x):
    return np.asarray(x).astype(np.float64)

E4M3FN = np.array([(-1.0 if i & 128 else 1.0) * ((1.0 + (i & 7) / 8.0) * 2.0 ** (((i >> 3) & 15) - 7) if i & 120 else (i & 7) * 2.0 ** -9) for i in range(256)])


def e4m3fn_bytes(y):
    return np.clip(np.asarray(y, np.float64), -448.0, 448.0).astype(np.float32).astype(ml_dtypes.float8_e4m3fn).view(np.uint8)


def e4m3fn_values(b):
    return E4M3FN[b]


T, D, R, B = 4096, 1024, 512, 128


def setup_inputs():
    s, t = mx_kscale(D), mx_kscale(R)
    c = f64(bf(1 + 0.1 * np.random.standard_normal(D)))
    z = np.random.standard_normal((T, D))
    v = np.linalg.svd(np.random.standard_normal((D, D)))[2][:R].T
    d = {"x": bf(z / c * s),
         "g": bf(c / s),
         "a": bf((1 + 0.1 * np.random.standard_normal(R)) * t)}
    for name, w in (("w1", v * (c / s)[:, None]), ("w2", v / t)):
        scale = (np.abs(w).reshape(D // B, B, R // B, B).max(axis=(1, 3)) / 448).astype(np.float32)
        d[name + "_bytes"] = e4m3fn_bytes(w / np.repeat(np.repeat(f64(scale), B, axis=0), B, axis=1))
        d[name + "_scale"] = scale
    return d


def reference(x, g, a, w1_bytes, w1_scale, w2_bytes, w2_scale):
    x = f64(x)
    w1 = e4m3fn_values(w1_bytes) * np.repeat(np.repeat(f64(w1_scale), B, axis=0), B, axis=1)
    w2 = e4m3fn_values(w2_bytes) * np.repeat(np.repeat(f64(w2_scale), B, axis=0), B, axis=1)
    h = (mxq(x, 1, "e4m3") @ mxq(w1, 0, "e4m3")) * f64(a)
    y = mxq(h, 1, "e4m3") @ mxq(w2, 1, "e4m3").T
    e = x * f64(g) - y
    return e * e

@@ -1,0 +1,367 @@
+from contextlib import ExitStack
+
+import concourse.mybir as mybir
+from concourse.masks import make_identity
+
+T, D, R = 4096, 1024, 512
+FLOPS = 4 * T * D * R
+
+F32 = mybir.dt.float32
+BF16 = mybir.dt.bfloat16
+U32 = mybir.dt.uint32
+U8 = mybir.dt.uint8
+E4M3 = mybir.dt.float8_e4m3fn
+X4 = mybir.dt.float8_e4m3fn_x4
+ALU = mybir.AluOpType
+ACT = mybir.ActivationFunctionType
+
+P = 128
+PAIRS = T // 256
+AHEAD = 8
+
+
+def tile_sensor_residual_squared_d7_kernel(tc, x, g, a, w1_bytes, w1_scale, w2_bytes, w2_scale, out):
+    nc = tc.nc
+    x_pairs = x.rearrange("(b p r) d -> b p (r d)", p=P, r=2)
+    out_pairs = out.rearrange("(b p r) d -> b p r d", p=P, r=2)
+
+    with ExitStack() as ctx:
+        keep = ctx.enter_context(tc.tile_pool(name="keep", bufs=1))
+        x_pool = ctx.enter_context(tc.tile_pool(name="x_pool", bufs=AHEAD + 2))
+        work = ctx.enter_context(tc.tile_pool(name="work", bufs=3))
+        psum = ctx.enter_context(tc.psum_pool(name="psum", bufs=2))
+        ctx.enter_context(tc.manual_schedule())
+
+        x_raw, x_laced, x_codes, x_scales = {}, {}, {}, {}
+        h_sums, h_laced, h_codes, h_scales = {}, {}, {}, {}
+        y_sums, xg, turned, result = {}, {}, {}, {}
+
+        def load_x(b):
+            tile = x_pool.tile([P, 2, D], BF16, name="x_tile", align_bytes=64)
+            nc.sync.dma_start(out=tile[:].rearrange("p r d -> p (r d)"), in_=x_pairs[b])
+            x_raw[b] = tile
+
+        scales_all = keep.tile([P, 2, 32], F32, name="scales_all")
+        nc.scalar.dma_start(out=scales_all[:, 0, :], in_=w1_scale.rearrange("i j -> (i j)").partition_broadcast(P))
+        w1_raw = keep.tile([P, 2, 4 * R], U8, name="w1_raw", align_bytes=64)
+        w2_raw = keep.tile([P, 2, 4 * R], U8, name="w2_raw", align_bytes=64)
+        w1_rows = w1_bytes.rearrange("(c p t) n -> p c (t n)", p=P, t=4)
+        w2_rows = w2_bytes.rearrange("(c p t) k -> p c (t k)", p=P, t=4)
+        for c in range(2):
+            nc.sync.dma_start(out=w1_raw[:, c, :], in_=w1_rows[:, c, :])
+        nc.scalar.dma_start(out=scales_all[:, 1, :], in_=w2_scale.rearrange("i j -> (i j)").partition_broadcast(P))
+        a_cols = keep.tile([P, 4], BF16, name="a_cols")
+        nc.scalar.dma_start(out=a_cols[:], in_=a.rearrange("(p t) -> p t", t=4))
+        g_cols = keep.tile([P, 2, 4], BF16, name="g_cols")
+        nc.scalar.dma_start(out=g_cols[:], in_=g.rearrange("(c p t) -> p c t", p=P, t=4))
+        load_x(0)
+        for c in range(2):
+            nc.sync.dma_start(out=w2_raw[:, c, :], in_=w2_rows[:, c, :])
+        for b in range(1, AHEAD):
+            load_x(b)
+        g_rows = keep.tile([P, D], BF16, name="g_rows", align_bytes=64)
+        nc.sync.dma_start(out=g_rows[:], in_=g.partition_broadcast(P))
+        g_rows_late = keep.tile([P, D], BF16, name="g_rows_late", align_bytes=64)
+
+        ident = keep.tile([P, P], F32, name="ident", align_bytes=64)
+        make_identity(nc, ident[:])
+
+        scale_cols = keep.tile([P, 2, 2, 4], F32, name="scale_cols")
+        for q in range(4):
+            quadrant = slice(32 * q, 32 * q + 32)
+            nc.vector.tensor_copy(
+                out=scale_cols[quadrant],
+                in_=scales_all[quadrant].rearrange("p w (c q j) -> p w c q j", q=4, j=4)[:, :, :, q, :],
+            )
+
+        w1_wide = keep.tile([P, 2, 4, R], BF16, name="w1_wide", align_bytes=64)
+        w1_laced = keep.tile([P, 2, 4, P, 4], BF16, name="w1_laced", align_bytes=64)
+        w1_codes = keep.tile([P, 2, R], U32, name="w1_codes", align_bytes=64)
+        w1_scales = keep.tile([P, 2, R], U8, name="w1_scales", align_bytes=64)
+        w2_wide = keep.tile([P, 2, 4, R], BF16, name="w2_wide", align_bytes=64)
+        w2_scaled = keep.tile([P, 2, 4, R], BF16, name="w2_scaled", align_bytes=64)
+        w2_laced = keep.tile([P, 2, 4, P, 4], BF16, name="w2_laced", align_bytes=64)
+        w2_codes = keep.tile([P, 2, R], U32, name="w2_codes", align_bytes=64)
+        w2_scales = keep.tile([P, 2, R], U8, name="w2_scales", align_bytes=64)
+
+        def widen(copy, wide, raw, c):
+            copy(out=wide[:, c, :, :].rearrange("p t n -> p (t n)"), in_=raw[:, c, :].bitcast(E4M3))
+
+        def lace_w1(c, j, on_scalar):
+            out_ = w1_laced[:, c, :, 32 * j : 32 * j + 32, :]
+            in_ = w1_wide[:, c, :, 128 * j : 128 * j + 128].rearrange("p t (m u) -> p u m t", u=4)
+            scale = scale_cols[:, 0, c, j : j + 1]
+            if on_scalar:
+                nc.scalar.activation(out=out_, in_=in_, func=ACT.Copy, scale=scale)
+            else:
+                nc.vector.tensor_scalar(out=out_, in0=in_, scalar1=scale, scalar2=None, op0=ALU.mult)
+
+        def scale_w2(c):
+            for j in range(4):
+                columns = slice(128 * j, 128 * j + 128)
+                nc.vector.tensor_scalar(
+                    out=w2_scaled[:, c, :, columns],
+                    in0=w2_wide[:, c, :, columns],
+                    scalar1=scale_cols[:, 1, c, j : j + 1],
+                    scalar2=None,
+                    op0=ALU.mult,
+                )
+
+        def turn_w2(c):
+            for half in range(2):
+                bank = psum.tile([P, 2, 2, P], F32, name="w2_bank", tag="x_turned")
+                for t in range(2):
+                    words = w2_scaled[:, c, 2 * half + t, :].bitcast(F32)
+                    for u in range(2):
+                        nc.tensor.transpose(bank[:, t, u, :], words[:, u::2], ident[:])
+                nc.scalar.copy(
+                    out=w2_laced[:, c, 2 * half : 2 * half + 2, :, :].bitcast(F32),
+                    in_=bank[:].rearrange("p t u m -> p t m u"),
+                )
+
+        def quantize_w(codes, scales, laced, c):
+            nc.vector.quantize_mx(
+                out=codes[:, c, :].bitcast(X4),
+                scales=scales[:, c, :],
+                in_=laced[:, c].rearrange("p u m t -> p (u m t)"),
+            )
+
+        def turn_x(b, r):
+            if r == 0:
+                x_laced[b] = work.tile([P, 2, 256, 4], BF16, name="x_laced_tile", align_bytes=64, bufs=8)
+            bank = psum.tile([P, 2, 2, P], F32, name="x_bank", tag="x_turned")
+            words = x_raw[b][:, r, :].bitcast(F32)
+            for c in range(2):
+                for u in range(2):
+                    nc.tensor.transpose(bank[:, c, u, :], words[:, 256 * c + u : 256 * (c + 1) : 2], ident[:])
+            nc.scalar.copy(
+                out=x_laced[b][:, :, 128 * r : 128 * r + 128, :].bitcast(F32),
+                in_=bank[:].rearrange("p c u n -> p c n u"),
+            )
+
+        def quantize_x(b):
+            x_codes[b] = work.tile([P, 2, 256], U32, name="x_codes_tile", align_bytes=64)
+            x_scales[b] = work.tile([P, 2, 256], U8, name="x_scales_tile", align_bytes=64)
+            nc.vector.quantize_mx(
+                out=x_codes[b][:].rearrange("p c n -> p (c n)").bitcast(X4),
+                scales=x_scales[b][:].rearrange("p c n -> p (c n)"),
+                in_=x_laced[b][:].rearrange("p c n t -> p (c n t)"),
+            )
+
+        def first_product(b, r):
+            bank = psum.tile([P, 4, P], F32, name="h_bank", tag="h_sums")
+            tokens = slice(128 * r, 128 * r + 128)
+            for u in range(4):
+                columns = slice(128 * u, 128 * u + 128)
+                for c in range(2):
+                    nc.tensor.matmul_mx(
+                        out=bank[:, u, :],
+                        lhsT=w1_codes[:, c, columns].bitcast(X4),
+                        lhsT_scale=w1_scales[:, c, columns],
+                        rhs=x_codes[b][:, c, tokens].bitcast(X4),
+                        rhs_scale=x_scales[b][:, c, tokens],
+                        start=(c == 0),
+                        stop=(c == 1),
+                    )
+            h_sums[b, r] = bank
+
+        def weigh(b, r):
+            if r == 0:
+                h_laced[b] = work.tile([P, 2, P, 4], BF16, name="h_laced_tile", align_bytes=64)
+            nc.vector.tensor_tensor(
+                out=h_laced[b][:, r, :, :],
+                in0=h_sums[b, r][:].rearrange("p u n -> p n u"),
+                in1=a_cols[:].unsqueeze(1).to_broadcast([P, P, 4]),
+                op=ALU.mult,
+            )
+
+        def quantize_h(b):
+            h_codes[b] = work.tile([P, 256], U32, name="h_codes_tile", align_bytes=64, bufs=4)
+            h_scales[b] = work.tile([P, 256], U8, name="h_scales_tile", align_bytes=64, bufs=4)
+            nc.vector.quantize_mx(
+                out=h_codes[b][:].bitcast(X4),
+                scales=h_scales[b][:],
+                in_=h_laced[b][:].rearrange("p r n t -> p (r n t)"),
+            )
+
+        def result_of(b):
+            if b not in result:
+                result[b] = work.tile([P, 2, D], F32, name="result_tile", align_bytes=64, bufs=4)
+            return result[b]
+
+        def standardise(b, r, engine, factors):
+            product = work.tile([P, D], F32, name="xg_tile", align_bytes=64, bufs=2)
+            engine.tensor_tensor(out=product[:], in0=x_raw[b][:, r, :], in1=factors[:], op=ALU.mult)
+            xg[b, r] = product
+
+        def product_direct(b, r):
+            tokens = slice(128 * r, 128 * r + 128)
+            for c in range(2):
+                bank = psum.tile([P, 4, P], F32, name="y_bank", tag="y_direct")
+                nc.tensor.matmul_mx(
+                    out=bank[:].rearrange("p t m -> p (t m)"),
+                    lhsT=h_codes[b][:, tokens].bitcast(X4),
+                    lhsT_scale=h_scales[b][:, tokens],
+                    rhs=w2_codes[:, c, :].bitcast(X4),
+                    rhs_scale=w2_scales[:, c, :],
+                    start=True,
+                    stop=True,
+                )
+                y_sums[b, r, c] = bank
+
+        def subtract_direct(b, r, c):
+            sensors = slice(512 * c, 512 * c + 512)
+            nc.vector.tensor_tensor(
+                out=result_of(b)[:, r, sensors].rearrange("p (m t) -> p m t", t=4),
+                in0=xg[b, r][:, sensors].rearrange("p (m t) -> p m t", t=4),
+                in1=y_sums[b, r, c][:].rearrange("p t m -> p m t"),
+                op=ALU.subtract,
+            )
+
+        def square_and_store(b, r):
+            tile = result[b][:, r, :]
+            if (b, r) != (PAIRS - 1, 1):
+                nc.scalar.activation(out=tile, in_=tile, func=ACT.Square)
+                nc.sync.dma_start(out=out_pairs[b][:, r, :], in_=tile)
+                return
+            nc.scalar.activation(out=tile[:, 0:512], in_=tile[:, 0:512], func=ACT.Square)
+            nc.sync.dma_start(out=out_pairs[b][:, r, 0:512], in_=tile[:, 0:512])
+            nc.vector.tensor_tensor(out=tile[:, 512:], in0=tile[:, 512:], in1=tile[:, 512:], op=ALU.mult)
+            nc.sync.dma_start(out=out_pairs[b][:, r, 512:], in_=tile[:, 512:])
+
+        def product_turned(b, c):
+            for i in range(2):
+                bank = psum.tile([P, 2, 256], F32, name="yt_bank", tag="y_turned")
+                for k in range(2):
+                    columns = slice(128 * (2 * i + k), 128 * (2 * i + k) + 128)
+                    nc.tensor.matmul_mx(
+                        out=bank[:, k, :],
+                        lhsT=w2_codes[:, c, columns].bitcast(X4),
+                        lhsT_scale=w2_scales[:, c, columns],
+                        rhs=h_codes[b][:].bitcast(X4),
+                        rhs_scale=h_scales[b][:],
+                        start=True,
+                        stop=True,
+                    )
+                y_sums[b, c, i] = bank
+
+        def subtract_turned(b, c, i):
+            if i == 0:
+                turned[b, c] = work.tile([P, 4, 256], F32, name="turned_tile", align_bytes=64, bufs=4)
+            for k in range(2):
+                t = 2 * i + k
+                nc.vector.scalar_tensor_tensor(
+                    out=turned[b, c][:, t, :],
+                    in0=x_laced[b][:, c, :, t],
+                    scalar=g_cols[:, c, t : t + 1],
+                    in1=y_sums[b, c, i][:, k, :],
+                    op0=ALU.mult,
+                    op1=ALU.subtract,
+                )
+
+        def turn_back(b, c, r):
+            bank = psum.tile([P, 4, P], F32, name="back_bank", tag="y_turned")
+            for t in range(4):
+                nc.tensor.transpose(bank[:, t, :], turned[b, c][:, t, 128 * r : 128 * r + 128], ident[:])
+            sensors = slice(512 * c, 512 * c + 512)
+            nc.scalar.activation(
+                out=result_of(b)[:, r, sensors].rearrange("p (m t) -> p m t", t=4),
+                in_=bank[:].rearrange("p t m -> p m t"),
+                func=ACT.Square,
+            )
+            if r == 1:
+                nc.sync.dma_start(out=out_pairs[b][:, :, sensors], in_=result[b][:, :, sensors])
+
+        def inside(b):
+            return 0 <= b < PAIRS
+
+        def direct_tile(k):
+            return (2 * (k // 2) + 1, k % 2) if inside(k) else None
+
+        def turned_part(k):
+            return (2 * (k // 2), k % 2) if inside(k) else None
+
+        widen(nc.scalar.copy, w1_wide, w1_raw, 1)
+        for j in (2, 3):
+            lace_w1(1, j, on_scalar=True)
+        widen(nc.vector.tensor_copy, w1_wide, w1_raw, 0)
+        turn_x(0, 0)
+        turn_x(0, 1)
+        for j in (0, 1):
+            lace_w1(1, j, on_scalar=False)
+        widen(nc.scalar.copy, w2_wide, w2_raw, 0)
+        for j in range(4):
+            lace_w1(0, j, on_scalar=False)
+        turn_x(1, 0)
+        turn_x(1, 1)
+        quantize_w(w1_codes, w1_scales, w1_laced, 1)
+        quantize_x(0)
+        widen(nc.scalar.copy, w2_wide, w2_raw, 1)
+        quantize_w(w1_codes, w1_scales, w1_laced, 0)
+        scale_w2(0)
+        first_product(0, 0)
+        turn_x(2, 0)
+        quantize_x(1)
+        weigh(0, 0)
+        scale_w2(1)
+        turn_x(2, 1)
+        first_product(0, 1)
+        weigh(0, 1)
+        quantize_x(2)
+        turn_w2(0)
+        first_product(1, 0)
+        quantize_h(0)
+        standardise(*direct_tile(0), nc.vector, g_rows)
+        quantize_w(w2_codes, w2_scales, w2_laced, 0)
+        turn_w2(1)
+        first_product(1, 1)
+        weigh(1, 0)
+        weigh(1, 1)
+        quantize_w(w2_codes, w2_scales, w2_laced, 1)
+        turn_x(3, 0)
+        first_product(2, 0)
+        turn_x(3, 1)
+        first_product(2, 1)
+
+        for s in range(PAIRS + 1):
+            part, part_before = turned_part(s), turned_part(s - 1)
+            tile, tile_next = direct_tile(s - 1), direct_tile(s)
+            if inside(s + AHEAD):
+                load_x(s + AHEAD)
+            if tile:
+                subtract_direct(*tile, 0)
+            if part_before:
+                turn_back(*part_before, 0)
+            if s == 0:
+                nc.scalar.copy(out=g_rows_late[:], in_=g_rows[:])
+            if part_before:
+                turn_back(*part_before, 1)
+            if inside(s + 4):
+                turn_x(s + 4, 0)
+            if inside(s + 1):
+                quantize_h(s + 1)
+            if inside(s + 3):
+                quantize_x(s + 3)
+            if inside(s + 4):
+                turn_x(s + 4, 1)
+            if part:
+                product_turned(*part)
+            if tile:
+                subtract_direct(*tile, 1)
+            if inside(s + 2):
+                weigh(s + 2, 0)
+            if tile_next:
+                product_direct(*tile_next)
+            if inside(s + 2):
+                weigh(s + 2, 1)
+            if part:
+                subtract_turned(*part, 0)
+            if tile:
+                square_and_store(*tile)
+            if part:
+                subtract_turned(*part, 1)
+            if tile_next and s > 0:
+                standardise(*tile_next, nc.gpsimd, g_rows_late)
+            if inside(s + 3):
+                first_product(s + 3, 0)
+                first_product(s + 3, 1)

@@ -16,8 +16,10 @@ ALU = mybir.AluOpType
 ACT = mybir.ActivationFunctionType
 
 P = 128
+HALF = 512
 PAIRS = T // 256
-AHEAD = 8
+TURNED, DIRECT = 0, 1
+MX_BANKS, TURN_BANKS = 5, 3
 
 
 def tile_sensor_residual_squared_d7_kernel(tc, x, g, a, w1_bytes, w1_scale, w2_bytes, w2_scale, out):
@@ -27,117 +29,131 @@ def tile_sensor_residual_squared_d7_kernel(tc, x, g, a, w1_bytes, w1_scale, w2_b
 
     with ExitStack() as ctx:
         keep = ctx.enter_context(tc.tile_pool(name="keep", bufs=1))
-        x_pool = ctx.enter_context(tc.tile_pool(name="x_pool", bufs=AHEAD + 2))
         work = ctx.enter_context(tc.tile_pool(name="work", bufs=3))
-        psum = ctx.enter_context(tc.psum_pool(name="psum", bufs=2))
+        psum = ctx.enter_context(tc.psum_pool(name="psum", bufs=1))
         ctx.enter_context(tc.manual_schedule())
 
         x_raw, x_laced, x_codes, x_scales = {}, {}, {}, {}
-        h_sums, h_laced, h_codes, h_scales = {}, {}, {}, {}
-        y_sums, xg, turned, result = {}, {}, {}, {}
+        h_sums, scratch, h_codes, h_scales = {}, {}, {}, {}
+        y_turned, y_direct, e_turned, result = {}, {}, {}, {}
+
+        def mx_bank(shape):
+            return psum.tile(shape, F32, name="mx_bank", bufs=MX_BANKS)
+
+        def turn_bank(shape):
+            return psum.tile(shape, F32, name="turn_bank", bufs=TURN_BANKS)
 
         def load_x(b):
-            tile = x_pool.tile([P, 2, D], BF16, name="x_tile", align_bytes=64)
+            tile = keep.tile([P, 2, D], BF16, name="x_tile", align_bytes=64, bufs=PAIRS)
             nc.sync.dma_start(out=tile[:].rearrange("p r d -> p (r d)"), in_=x_pairs[b])
             x_raw[b] = tile
 
-        scales_all = keep.tile([P, 2, 32], F32, name="scales_all")
-        nc.scalar.dma_start(out=scales_all[:, 0, :], in_=w1_scale.rearrange("i j -> (i j)").partition_broadcast(P))
-        w1_raw = keep.tile([P, 2, 4 * R], U8, name="w1_raw", align_bytes=64)
-        w2_raw = keep.tile([P, 2, 4 * R], U8, name="w2_raw", align_bytes=64)
-        w1_rows = w1_bytes.rearrange("(c p t) n -> p c (t n)", p=P, t=4)
-        w2_rows = w2_bytes.rearrange("(c p t) k -> p c (t k)", p=P, t=4)
-        for c in range(2):
-            nc.sync.dma_start(out=w1_raw[:, c, :], in_=w1_rows[:, c, :])
-        nc.scalar.dma_start(out=scales_all[:, 1, :], in_=w2_scale.rearrange("i j -> (i j)").partition_broadcast(P))
+        scales_all = [keep.tile([P, 32], F32, name="scales_all", bufs=2) for w in range(2)]
+        w_raw = {(w, c): keep.tile([P, 4 * R], U8, name="w_raw", align_bytes=64, bufs=4) for w in range(2) for c in range(2)}
+        w_rows = [bytes_in.rearrange("(c p t) n -> p c (t n)", p=P, t=4) for bytes_in in (w1_bytes, w2_bytes)]
         a_cols = keep.tile([P, 4], BF16, name="a_cols")
-        nc.scalar.dma_start(out=a_cols[:], in_=a.rearrange("(p t) -> p t", t=4))
-        g_cols = keep.tile([P, 2, 4], BF16, name="g_cols")
-        nc.scalar.dma_start(out=g_cols[:], in_=g.rearrange("(c p t) -> p c t", p=P, t=4))
-        load_x(0)
+        g_cols = keep.tile([P, 4], BF16, name="g_cols")
+        g_rows = keep.tile([P, HALF], BF16, name="g_rows", align_bytes=64)
+
+        nc.scalar.dma_start(out=scales_all[0][:], in_=w1_scale.rearrange("i j -> (i j)").partition_broadcast(P))
         for c in range(2):
-            nc.sync.dma_start(out=w2_raw[:, c, :], in_=w2_rows[:, c, :])
-        for b in range(1, AHEAD):
+            nc.sync.dma_start(out=w_raw[0, c][:], in_=w_rows[0][:, c, :])
+        nc.scalar.dma_start(out=scales_all[1][:], in_=w2_scale.rearrange("i j -> (i j)").partition_broadcast(P))
+        load_x(0)
+        nc.sync.dma_start(out=w_raw[1, 0][:], in_=w_rows[1][:, 0, :])
+        load_x(1)
+        nc.sync.dma_start(out=w_raw[1, 1][:], in_=w_rows[1][:, 1, :])
+        nc.sync.dma_start(out=a_cols[:], in_=a.rearrange("(p t) -> p t", t=4))
+        load_x(2)
+        nc.sync.dma_start(out=g_rows[:], in_=g[HALF:].partition_broadcast(P))
+        nc.sync.dma_start(out=g_cols[:], in_=g[0:HALF].rearrange("(p t) -> p t", t=4))
+        for b in range(3, PAIRS):
             load_x(b)
-        g_rows = keep.tile([P, D], BF16, name="g_rows", align_bytes=64)
-        nc.sync.dma_start(out=g_rows[:], in_=g.partition_broadcast(P))
-        g_rows_late = keep.tile([P, D], BF16, name="g_rows_late", align_bytes=64)
 
         ident = keep.tile([P, P], F32, name="ident", align_bytes=64)
         make_identity(nc, ident[:])
 
-        scale_cols = keep.tile([P, 2, 2, 4], F32, name="scale_cols")
-        for q in range(4):
-            quadrant = slice(32 * q, 32 * q + 32)
-            nc.vector.tensor_copy(
-                out=scale_cols[quadrant],
-                in_=scales_all[quadrant].rearrange("p w (c q j) -> p w c q j", q=4, j=4)[:, :, :, q, :],
-            )
+        scale_cols = [keep.tile([P, 2, 4], F32, name="scale_cols", bufs=2) for w in range(2)]
+        wide, laced, w2_scaled = {}, {}, {}
+        w_codes = [keep.tile([P, 2, R], U32, name="w_codes", align_bytes=64, bufs=2) for w in range(2)]
+        w_scales = [keep.tile([P, 2, R], U8, name="w_scales", align_bytes=64, bufs=2) for w in range(2)]
 
-        w1_wide = keep.tile([P, 2, 4, R], BF16, name="w1_wide", align_bytes=64)
-        w1_laced = keep.tile([P, 2, 4, P, 4], BF16, name="w1_laced", align_bytes=64)
-        w1_codes = keep.tile([P, 2, R], U32, name="w1_codes", align_bytes=64)
-        w1_scales = keep.tile([P, 2, R], U8, name="w1_scales", align_bytes=64)
-        w2_wide = keep.tile([P, 2, 4, R], BF16, name="w2_wide", align_bytes=64)
-        w2_scaled = keep.tile([P, 2, 4, R], BF16, name="w2_scaled", align_bytes=64)
-        w2_laced = keep.tile([P, 2, 4, P, 4], BF16, name="w2_laced", align_bytes=64)
-        w2_codes = keep.tile([P, 2, R], U32, name="w2_codes", align_bytes=64)
-        w2_scales = keep.tile([P, 2, R], U8, name="w2_scales", align_bytes=64)
+        def pick_scales(w):
+            for q in range(4):
+                quadrant = slice(32 * q, 32 * q + 32)
+                nc.vector.tensor_copy(
+                    out=scale_cols[w][quadrant],
+                    in_=scales_all[w][quadrant].rearrange("p (c q j) -> p c q j", q=4, j=4)[:, :, q, :],
+                )
 
-        def widen(copy, wide, raw, c):
-            copy(out=wide[:, c, :, :].rearrange("p t n -> p (t n)"), in_=raw[:, c, :].bitcast(E4M3))
+        def widen(copy, w, c):
+            wide[w, c] = keep.tile([P, 4, R], BF16, name="wide", align_bytes=64, bufs=4)
+            copy(out=wide[w, c][:].rearrange("p t n -> p (t n)"), in_=w_raw[w, c][:].bitcast(E4M3))
+
+        def laced_of(w, c):
+            if (w, c) not in laced:
+                laced[w, c] = keep.tile([P, R, 4], BF16, name="laced", align_bytes=64, bufs=4)
+            return laced[w, c]
 
         def lace_w1(c, j, on_scalar):
-            out_ = w1_laced[:, c, :, 32 * j : 32 * j + 32, :]
-            in_ = w1_wide[:, c, :, 128 * j : 128 * j + 128].rearrange("p t (m u) -> p u m t", u=4)
-            scale = scale_cols[:, 0, c, j : j + 1]
+            out_ = laced_of(0, c)[:].rearrange("p (u m) t -> p u m t", u=4)[:, :, 32 * j : 32 * j + 32, :]
+            in_ = wide[0, c][:, :, 128 * j : 128 * j + 128].rearrange("p t (m u) -> p u m t", u=4)
+            scale = scale_cols[0][:, c, j : j + 1]
             if on_scalar:
                 nc.scalar.activation(out=out_, in_=in_, func=ACT.Copy, scale=scale)
             else:
                 nc.vector.tensor_scalar(out=out_, in0=in_, scalar1=scale, scalar2=None, op0=ALU.mult)
 
         def scale_w2(c):
+            w2_scaled[c] = keep.tile([P, 4, R], BF16, name="w2_scaled", align_bytes=64, bufs=2)
             for j in range(4):
                 columns = slice(128 * j, 128 * j + 128)
                 nc.vector.tensor_scalar(
-                    out=w2_scaled[:, c, :, columns],
-                    in0=w2_wide[:, c, :, columns],
-                    scalar1=scale_cols[:, 1, c, j : j + 1],
+                    out=w2_scaled[c][:, :, columns],
+                    in0=wide[1, c][:, :, columns],
+                    scalar1=scale_cols[1][:, c, j : j + 1],
                     scalar2=None,
                     op0=ALU.mult,
                 )
 
         def turn_w2(c):
-            for half in range(2):
-                bank = psum.tile([P, 2, 2, P], F32, name="w2_bank", tag="x_turned")
-                for t in range(2):
-                    words = w2_scaled[:, c, 2 * half + t, :].bitcast(F32)
+            words_out = laced_of(1, c)[:].bitcast(F32)
+            for i in range(2):
+                bank = turn_bank([P, 2, 2, P])
+                for k in range(2):
+                    words = w2_scaled[c][:, 2 * i + k, :].bitcast(F32)
                     for u in range(2):
-                        nc.tensor.transpose(bank[:, t, u, :], words[:, u::2], ident[:])
-                nc.scalar.copy(
-                    out=w2_laced[:, c, 2 * half : 2 * half + 2, :, :].bitcast(F32),
-                    in_=bank[:].rearrange("p t u m -> p t m u"),
-                )
+                        nc.tensor.transpose(bank[:, k, u, :], words[:, u::2], ident[:])
+                if c == TURNED:
+                    nc.scalar.copy(
+                        out=words_out.rearrange("p (t m) u -> p t m u", t=4)[:, 2 * i : 2 * i + 2],
+                        in_=bank[:].rearrange("p k u m -> p k m u"),
+                    )
+                else:
+                    nc.scalar.copy(
+                        out=words_out.rearrange("p (m t) u -> p m t u", t=4)[:, :, 2 * i : 2 * i + 2, :],
+                        in_=bank[:].rearrange("p k u m -> p m k u"),
+                    )
 
-        def quantize_w(codes, scales, laced, c):
+        def quantize_w(w, c):
             nc.vector.quantize_mx(
-                out=codes[:, c, :].bitcast(X4),
-                scales=scales[:, c, :],
-                in_=laced[:, c].rearrange("p u m t -> p (u m t)"),
+                out=w_codes[w][:, c, :].bitcast(X4),
+                scales=w_scales[w][:, c, :],
+                in_=laced[w, c][:].rearrange("p n t -> p (n t)"),
             )
 
-        def turn_x(b, r):
-            if r == 0:
-                x_laced[b] = work.tile([P, 2, 256, 4], BF16, name="x_laced_tile", align_bytes=64, bufs=8)
-            bank = psum.tile([P, 2, 2, P], F32, name="x_bank", tag="x_turned")
-            words = x_raw[b][:, r, :].bitcast(F32)
-            for c in range(2):
-                for u in range(2):
-                    nc.tensor.transpose(bank[:, c, u, :], words[:, 256 * c + u : 256 * (c + 1) : 2], ident[:])
-            nc.scalar.copy(
-                out=x_laced[b][:, :, 128 * r : 128 * r + 128, :].bitcast(F32),
-                in_=bank[:].rearrange("p c u n -> p c n u"),
-            )
+        def turn_x(b):
+            x_laced[b] = work.tile([P, 2, 256, 4], BF16, name="x_laced_tile", align_bytes=64, bufs=6)
+            for r in range(2):
+                bank = turn_bank([P, 2, 2, P])
+                words = x_raw[b][:, r, :].bitcast(F32)
+                for c in range(2):
+                    for u in range(2):
+                        nc.tensor.transpose(bank[:, c, u, :], words[:, 256 * c + u : 256 * (c + 1) : 2], ident[:])
+                nc.scalar.copy(
+                    out=x_laced[b][:, :, 128 * r : 128 * r + 128, :].bitcast(F32),
+                    in_=bank[:].rearrange("p c u n -> p c n u"),
+                )
 
         def quantize_x(b):
             x_codes[b] = work.tile([P, 2, 256], U32, name="x_codes_tile", align_bytes=64)
@@ -149,15 +165,15 @@ def tile_sensor_residual_squared_d7_kernel(tc, x, g, a, w1_bytes, w1_scale, w2_b
             )
 
         def first_product(b, r):
-            bank = psum.tile([P, 4, P], F32, name="h_bank", tag="h_sums")
+            bank = mx_bank([P, 4, P])
             tokens = slice(128 * r, 128 * r + 128)
             for u in range(4):
                 columns = slice(128 * u, 128 * u + 128)
                 for c in range(2):
                     nc.tensor.matmul_mx(
                         out=bank[:, u, :],
-                        lhsT=w1_codes[:, c, columns].bitcast(X4),
-                        lhsT_scale=w1_scales[:, c, columns],
+                        lhsT=w_codes[0][:, c, columns].bitcast(X4),
+                        lhsT_scale=w_scales[0][:, c, columns],
                         rhs=x_codes[b][:, c, tokens].bitcast(X4),
                         rhs_scale=x_scales[b][:, c, tokens],
                         start=(c == 0),
@@ -165,203 +181,162 @@ def tile_sensor_residual_squared_d7_kernel(tc, x, g, a, w1_bytes, w1_scale, w2_b
                     )
             h_sums[b, r] = bank
 
+        def h_laced(b):
+            return scratch[b][:, 0, :].bitcast(BF16)
+
         def weigh(b, r):
             if r == 0:
-                h_laced[b] = work.tile([P, 2, P, 4], BF16, name="h_laced_tile", align_bytes=64)
+                scratch[b] = work.tile([P, 2, HALF], F32, name="scratch_tile", align_bytes=64)
             nc.vector.tensor_tensor(
-                out=h_laced[b][:, r, :, :],
+                out=h_laced(b).rearrange("p (r n t) -> p r n t", r=2, t=4)[:, r],
                 in0=h_sums[b, r][:].rearrange("p u n -> p n u"),
                 in1=a_cols[:].unsqueeze(1).to_broadcast([P, P, 4]),
                 op=ALU.mult,
             )
 
         def quantize_h(b):
-            h_codes[b] = work.tile([P, 256], U32, name="h_codes_tile", align_bytes=64, bufs=4)
-            h_scales[b] = work.tile([P, 256], U8, name="h_scales_tile", align_bytes=64, bufs=4)
-            nc.vector.quantize_mx(
-                out=h_codes[b][:].bitcast(X4),
-                scales=h_scales[b][:],
-                in_=h_laced[b][:].rearrange("p r n t -> p (r n t)"),
+            h_codes[b] = work.tile([P, 256], U32, name="h_codes_tile", align_bytes=64)
+            h_scales[b] = work.tile([P, 256], U8, name="h_scales_tile", align_bytes=64)
+            nc.vector.quantize_mx(out=h_codes[b][:].bitcast(X4), scales=h_scales[b][:], in_=h_laced(b))
+
+        def standardise(b):
+            nc.gpsimd.tensor_tensor(
+                out=scratch[b][:],
+                in0=x_raw[b][:, :, HALF:],
+                in1=g_rows[:].unsqueeze(1).to_broadcast([P, 2, HALF]),
+                op=ALU.mult,
             )
 
-        def result_of(b):
-            if b not in result:
-                result[b] = work.tile([P, 2, D], F32, name="result_tile", align_bytes=64, bufs=4)
-            return result[b]
-
-        def standardise(b, r, engine, factors):
-            product = work.tile([P, D], F32, name="xg_tile", align_bytes=64, bufs=2)
-            engine.tensor_tensor(out=product[:], in0=x_raw[b][:, r, :], in1=factors[:], op=ALU.mult)
-            xg[b, r] = product
-
-        def product_direct(b, r):
-            tokens = slice(128 * r, 128 * r + 128)
-            for c in range(2):
-                bank = psum.tile([P, 4, P], F32, name="y_bank", tag="y_direct")
+        def product_turned(b, i):
+            bank = mx_bank([P, 2, 256])
+            for k in range(2):
+                columns = slice(128 * (2 * i + k), 128 * (2 * i + k) + 128)
                 nc.tensor.matmul_mx(
-                    out=bank[:].rearrange("p t m -> p (t m)"),
-                    lhsT=h_codes[b][:, tokens].bitcast(X4),
-                    lhsT_scale=h_scales[b][:, tokens],
-                    rhs=w2_codes[:, c, :].bitcast(X4),
-                    rhs_scale=w2_scales[:, c, :],
+                    out=bank[:, k, :],
+                    lhsT=w_codes[1][:, TURNED, columns].bitcast(X4),
+                    lhsT_scale=w_scales[1][:, TURNED, columns],
+                    rhs=h_codes[b][:].bitcast(X4),
+                    rhs_scale=h_scales[b][:],
                     start=True,
                     stop=True,
                 )
-                y_sums[b, r, c] = bank
+            y_turned[b, i] = bank
 
-        def subtract_direct(b, r, c):
-            sensors = slice(512 * c, 512 * c + 512)
-            nc.vector.tensor_tensor(
-                out=result_of(b)[:, r, sensors].rearrange("p (m t) -> p m t", t=4),
-                in0=xg[b, r][:, sensors].rearrange("p (m t) -> p m t", t=4),
-                in1=y_sums[b, r, c][:].rearrange("p t m -> p m t"),
-                op=ALU.subtract,
-            )
-
-        def square_and_store(b, r):
-            tile = result[b][:, r, :]
-            if (b, r) != (PAIRS - 1, 1):
-                nc.scalar.activation(out=tile, in_=tile, func=ACT.Square)
-                nc.sync.dma_start(out=out_pairs[b][:, r, :], in_=tile)
-                return
-            nc.scalar.activation(out=tile[:, 0:512], in_=tile[:, 0:512], func=ACT.Square)
-            nc.sync.dma_start(out=out_pairs[b][:, r, 0:512], in_=tile[:, 0:512])
-            nc.vector.tensor_tensor(out=tile[:, 512:], in0=tile[:, 512:], in1=tile[:, 512:], op=ALU.mult)
-            nc.sync.dma_start(out=out_pairs[b][:, r, 512:], in_=tile[:, 512:])
-
-        def product_turned(b, c):
-            for i in range(2):
-                bank = psum.tile([P, 2, 256], F32, name="yt_bank", tag="y_turned")
-                for k in range(2):
-                    columns = slice(128 * (2 * i + k), 128 * (2 * i + k) + 128)
-                    nc.tensor.matmul_mx(
-                        out=bank[:, k, :],
-                        lhsT=w2_codes[:, c, columns].bitcast(X4),
-                        lhsT_scale=w2_scales[:, c, columns],
-                        rhs=h_codes[b][:].bitcast(X4),
-                        rhs_scale=h_scales[b][:],
-                        start=True,
-                        stop=True,
-                    )
-                y_sums[b, c, i] = bank
-
-        def subtract_turned(b, c, i):
+        def subtract_turned(b, i):
             if i == 0:
-                turned[b, c] = work.tile([P, 4, 256], F32, name="turned_tile", align_bytes=64, bufs=4)
+                e_turned[b] = work.tile([P, 4, 256], F32, name="e_turned_tile", align_bytes=64, bufs=2)
             for k in range(2):
                 t = 2 * i + k
                 nc.vector.scalar_tensor_tensor(
-                    out=turned[b, c][:, t, :],
-                    in0=x_laced[b][:, c, :, t],
-                    scalar=g_cols[:, c, t : t + 1],
-                    in1=y_sums[b, c, i][:, k, :],
+                    out=e_turned[b][:, t, :],
+                    in0=x_laced[b][:, TURNED, :, t],
+                    scalar=g_cols[:, t : t + 1],
+                    in1=y_turned[b, i][:, k, :],
                     op0=ALU.mult,
                     op1=ALU.subtract,
                 )
+            if i == 1:
+                result[b] = work.tile([P, 2, D], F32, name="result_tile", align_bytes=64)
 
-        def turn_back(b, c, r):
-            bank = psum.tile([P, 4, P], F32, name="back_bank", tag="y_turned")
+        def turn_back(b, r):
+            bank = turn_bank([P, 4, P])
             for t in range(4):
-                nc.tensor.transpose(bank[:, t, :], turned[b, c][:, t, 128 * r : 128 * r + 128], ident[:])
-            sensors = slice(512 * c, 512 * c + 512)
+                nc.tensor.transpose(bank[:, t, :], e_turned[b][:, t, 128 * r : 128 * r + 128], ident[:])
             nc.scalar.activation(
-                out=result_of(b)[:, r, sensors].rearrange("p (m t) -> p m t", t=4),
+                out=result[b][:, r, 0:HALF].rearrange("p (m t) -> p m t", t=4),
                 in_=bank[:].rearrange("p t m -> p m t"),
                 func=ACT.Square,
             )
-            if r == 1:
-                nc.sync.dma_start(out=out_pairs[b][:, :, sensors], in_=result[b][:, :, sensors])
+
+        def product_direct(b, r):
+            tokens = slice(128 * r, 128 * r + 128)
+            bank = mx_bank([P, HALF])
+            nc.tensor.matmul_mx(
+                out=bank[:],
+                lhsT=h_codes[b][:, tokens].bitcast(X4),
+                lhsT_scale=h_scales[b][:, tokens],
+                rhs=w_codes[1][:, DIRECT, :].bitcast(X4),
+                rhs_scale=w_scales[1][:, DIRECT, :],
+                start=True,
+                stop=True,
+            )
+            y_direct[b, r] = bank
+
+        def subtract_direct(b, r):
+            nc.vector.tensor_tensor(
+                out=result[b][:, r, HALF:], in0=scratch[b][:, r, :], in1=y_direct[b, r][:], op=ALU.subtract
+            )
+
+        def store(b, tiles, sensors):
+            nc.sync.dma_start(out=out_pairs[b][:, tiles, sensors], in_=result[b][:, tiles, sensors])
 
         def inside(b):
             return 0 <= b < PAIRS
 
-        def direct_tile(k):
-            return (2 * (k // 2) + 1, k % 2) if inside(k) else None
-
-        def turned_part(k):
-            return (2 * (k // 2), k % 2) if inside(k) else None
-
-        widen(nc.scalar.copy, w1_wide, w1_raw, 1)
+        widen(nc.vector.tensor_copy, 0, 0)
+        widen(nc.scalar.copy, 0, 1)
+        pick_scales(0)
         for j in (2, 3):
             lace_w1(1, j, on_scalar=True)
-        widen(nc.vector.tensor_copy, w1_wide, w1_raw, 0)
-        turn_x(0, 0)
-        turn_x(0, 1)
-        for j in (0, 1):
-            lace_w1(1, j, on_scalar=False)
-        widen(nc.scalar.copy, w2_wide, w2_raw, 0)
+        turn_x(0)
         for j in range(4):
             lace_w1(0, j, on_scalar=False)
-        turn_x(1, 0)
-        turn_x(1, 1)
-        quantize_w(w1_codes, w1_scales, w1_laced, 1)
-        quantize_x(0)
-        widen(nc.scalar.copy, w2_wide, w2_raw, 1)
-        quantize_w(w1_codes, w1_scales, w1_laced, 0)
-        scale_w2(0)
-        first_product(0, 0)
-        turn_x(2, 0)
-        quantize_x(1)
-        weigh(0, 0)
-        scale_w2(1)
-        turn_x(2, 1)
-        first_product(0, 1)
-        weigh(0, 1)
-        quantize_x(2)
-        turn_w2(0)
-        first_product(1, 0)
-        quantize_h(0)
-        standardise(*direct_tile(0), nc.vector, g_rows)
-        quantize_w(w2_codes, w2_scales, w2_laced, 0)
-        turn_w2(1)
-        first_product(1, 1)
-        weigh(1, 0)
-        weigh(1, 1)
-        quantize_w(w2_codes, w2_scales, w2_laced, 1)
-        turn_x(3, 0)
-        first_product(2, 0)
-        turn_x(3, 1)
-        first_product(2, 1)
+        for j in (0, 1):
+            lace_w1(1, j, on_scalar=False)
+        quantize_w(0, 0)
+        pick_scales(1)
+        quantize_w(0, 1)
 
-        for s in range(PAIRS + 1):
-            part, part_before = turned_part(s), turned_part(s - 1)
-            tile, tile_next = direct_tile(s - 1), direct_tile(s)
-            if inside(s + AHEAD):
-                load_x(s + AHEAD)
-            if tile:
-                subtract_direct(*tile, 0)
-            if part_before:
-                turn_back(*part_before, 0)
-            if s == 0:
-                nc.scalar.copy(out=g_rows_late[:], in_=g_rows[:])
-            if part_before:
-                turn_back(*part_before, 1)
-            if inside(s + 4):
-                turn_x(s + 4, 0)
-            if inside(s + 1):
-                quantize_h(s + 1)
+        both, last = slice(0, 2), PAIRS - 1
+        for s in range(-3, PAIRS):
+            if s in (-3, -2):
+                widen(nc.scalar.copy, 1, s + 3)
+            if inside(s):
+                for i in range(2):
+                    product_turned(s, i)
             if inside(s + 3):
                 quantize_x(s + 3)
+            if inside(s + 1):
+                quantize_h(s + 1)
+                standardise(s + 1)
+            if s in (-3, -2):
+                scale_w2(s + 3)
+            if inside(s + 2):
+                for r in range(2):
+                    first_product(s + 2, r)
+            if inside(s):
+                product_direct(s, 0)
+                subtract_turned(s, 0)
+                product_direct(s, 1)
+                subtract_turned(s, 1)
+            if inside(s + 2):
+                for r in range(2):
+                    weigh(s + 2, r)
+            if s == -1:
+                for c in range(2):
+                    quantize_w(1, c)
+            if inside(s):
+                for r in range(2):
+                    subtract_direct(s, r)
             if inside(s + 4):
-                turn_x(s + 4, 1)
-            if part:
-                product_turned(*part)
-            if tile:
-                subtract_direct(*tile, 1)
-            if inside(s + 2):
-                weigh(s + 2, 0)
-            if tile_next:
-                product_direct(*tile_next)
-            if inside(s + 2):
-                weigh(s + 2, 1)
-            if part:
-                subtract_turned(*part, 0)
-            if tile:
-                square_and_store(*tile)
-            if part:
-                subtract_turned(*part, 1)
-            if tile_next and s > 0:
-                standardise(*tile_next, nc.gpsimd, g_rows_late)
-            if inside(s + 3):
-                first_product(s + 3, 0)
-                first_product(s + 3, 1)
+                turn_x(s + 4)
+            if s == -2:
+                for c in range(2):
+                    turn_w2(c)
+            if inside(s) and s < last:
+                for r in range(2):
+                    turn_back(s, r)
+                store(s, both, slice(0, HALF))
+                tile = result[s][:, :, HALF:]
+                nc.scalar.activation(out=tile, in_=tile, func=ACT.Square)
+                store(s, both, slice(HALF, D))
+
+        for r in range(2):
+            turn_back(last, r)
+            store(last, r, slice(0, HALF))
+        tile = result[last][:, 0, HALF:]
+        nc.vector.tensor_tensor(out=tile, in0=tile, in1=tile, op=ALU.mult)
+        store(last, 0, slice(HALF, D))
+        tile = result[last][:, 1, HALF:]
+        nc.scalar.activation(out=tile, in_=tile, func=ACT.Square)
+        store(last, 1, slice(HALF, D))

@@ -19,7 +19,8 @@ P = 128
 HALF = 512
 PAIRS = T // 256
 TURNED, DIRECT = 0, 1
-MX_BANKS, TURN_BANKS = 5, 3
+MX_BANKS, TURN_BANKS = 4, 4
+SORTED_FROM = 6
 
 
 def tile_sensor_residual_squared_d7_kernel(tc, x, g, a, w1_bytes, w1_scale, w2_bytes, w2_scale, out):
@@ -33,7 +34,7 @@ def tile_sensor_residual_squared_d7_kernel(tc, x, g, a, w1_bytes, w1_scale, w2_b
         psum = ctx.enter_context(tc.psum_pool(name="psum", bufs=1))
         ctx.enter_context(tc.manual_schedule())
 
-        x_raw, x_laced, x_codes, x_scales = {}, {}, {}, {}
+        x_raw, x_sorted, x_laced, x_codes, x_scales = {}, {}, {}, {}, {}
         h_sums, scratch, h_codes, h_scales = {}, {}, {}, {}
         y_turned, y_direct, e_turned, result = {}, {}, {}, {}
 
@@ -59,15 +60,15 @@ def tile_sensor_residual_squared_d7_kernel(tc, x, g, a, w1_bytes, w1_scale, w2_b
         for c in range(2):
             nc.sync.dma_start(out=w_raw[0, c][:], in_=w_rows[0][:, c, :])
         nc.scalar.dma_start(out=scales_all[1][:], in_=w2_scale.rearrange("i j -> (i j)").partition_broadcast(P))
-        load_x(0)
+        for b in range(3):
+            load_x(b)
         nc.sync.dma_start(out=w_raw[1, 0][:], in_=w_rows[1][:, 0, :])
-        load_x(1)
-        nc.sync.dma_start(out=w_raw[1, 1][:], in_=w_rows[1][:, 1, :])
         nc.sync.dma_start(out=a_cols[:], in_=a.rearrange("(p t) -> p t", t=4))
-        load_x(2)
+        nc.sync.dma_start(out=w_raw[1, 1][:], in_=w_rows[1][:, 1, :])
+        load_x(3)
         nc.sync.dma_start(out=g_rows[:], in_=g[HALF:].partition_broadcast(P))
         nc.sync.dma_start(out=g_cols[:], in_=g[0:HALF].rearrange("(p t) -> p t", t=4))
-        for b in range(3, PAIRS):
+        for b in range(4, PAIRS):
             load_x(b)
 
         ident = keep.tile([P, P], F32, name="ident", align_bytes=64)
@@ -142,18 +143,35 @@ def tile_sensor_residual_squared_d7_kernel(tc, x, g, a, w1_bytes, w1_scale, w2_b
                 in_=laced[w, c][:].rearrange("p n t -> p (n t)"),
             )
 
-        def turn_x(b):
-            x_laced[b] = work.tile([P, 2, 256, 4], BF16, name="x_laced_tile", align_bytes=64, bufs=6)
+        def sort_x(b, r):
+            tile = work.tile([P, 2, 2, P], F32, name="x_sorted_tile", align_bytes=64)
+            words = x_raw[b][:, r, :].bitcast(F32)
+            nc.scalar.copy(out=tile[:], in_=words.rearrange("p (c m u) -> p c u m", c=2, u=2))
+            x_sorted[b, r] = tile
+
+        def turn_x(b, r):
+            bank = turn_bank([P, 2, 2, P])
+            words = x_raw[b][:, r, :].bitcast(F32)
+            for c in range(2):
+                for u in range(2):
+                    if (b, r) in x_sorted:
+                        source = x_sorted[b, r][:, c, u, :]
+                    else:
+                        source = words[:, 256 * c + u : 256 * (c + 1) : 2]
+                    nc.tensor.transpose(bank[:, c, u, :], source, ident[:])
+            return bank
+
+        def lace_x(b, r, bank):
+            if r == 0:
+                x_laced[b] = work.tile([P, 2, 256, 4], BF16, name="x_laced_tile", align_bytes=64, bufs=7)
+            nc.scalar.copy(
+                out=x_laced[b][:, :, 128 * r : 128 * r + 128, :].bitcast(F32),
+                in_=bank[:].rearrange("p c u n -> p c n u"),
+            )
+
+        def turn_and_lace_x(b):
             for r in range(2):
-                bank = turn_bank([P, 2, 2, P])
-                words = x_raw[b][:, r, :].bitcast(F32)
-                for c in range(2):
-                    for u in range(2):
-                        nc.tensor.transpose(bank[:, c, u, :], words[:, 256 * c + u : 256 * (c + 1) : 2], ident[:])
-                nc.scalar.copy(
-                    out=x_laced[b][:, :, 128 * r : 128 * r + 128, :].bitcast(F32),
-                    in_=bank[:].rearrange("p c u n -> p c n u"),
-                )
+                lace_x(b, r, turn_x(b, r))
 
         def quantize_x(b):
             x_codes[b] = work.tile([P, 2, 256], U32, name="x_codes_tile", align_bytes=64)
@@ -181,12 +199,15 @@ def tile_sensor_residual_squared_d7_kernel(tc, x, g, a, w1_bytes, w1_scale, w2_b
                     )
             h_sums[b, r] = bank
 
+        def new_scratch(b):
+            scratch[b] = work.tile([P, 2, HALF], F32, name="scratch_tile", align_bytes=64, bufs=4)
+
         def h_laced(b):
             return scratch[b][:, 0, :].bitcast(BF16)
 
         def weigh(b, r):
             if r == 0:
-                scratch[b] = work.tile([P, 2, HALF], F32, name="scratch_tile", align_bytes=64)
+                new_scratch(b)
             nc.vector.tensor_tensor(
                 out=h_laced(b).rearrange("p (r n t) -> p r n t", r=2, t=4)[:, r],
                 in0=h_sums[b, r][:].rearrange("p u n -> p n u"),
@@ -195,13 +216,13 @@ def tile_sensor_residual_squared_d7_kernel(tc, x, g, a, w1_bytes, w1_scale, w2_b
             )
 
         def quantize_h(b):
-            h_codes[b] = work.tile([P, 256], U32, name="h_codes_tile", align_bytes=64)
-            h_scales[b] = work.tile([P, 256], U8, name="h_scales_tile", align_bytes=64)
+            h_codes[b] = work.tile([P, 256], U32, name="h_codes_tile", align_bytes=64, bufs=4)
+            h_scales[b] = work.tile([P, 256], U8, name="h_scales_tile", align_bytes=64, bufs=4)
             nc.vector.quantize_mx(out=h_codes[b][:].bitcast(X4), scales=h_scales[b][:], in_=h_laced(b))
 
         def standardise(b):
             nc.gpsimd.tensor_tensor(
-                out=scratch[b][:],
+                out=scratch[b + 1][:],
                 in0=x_raw[b][:, :, HALF:],
                 in1=g_rows[:].unsqueeze(1).to_broadcast([P, 2, HALF]),
                 op=ALU.mult,
@@ -235,10 +256,10 @@ def tile_sensor_residual_squared_d7_kernel(tc, x, g, a, w1_bytes, w1_scale, w2_b
                     op0=ALU.mult,
                     op1=ALU.subtract,
                 )
-            if i == 1:
-                result[b] = work.tile([P, 2, D], F32, name="result_tile", align_bytes=64)
 
         def turn_back(b, r):
+            if r == 0:
+                result[b] = work.tile([P, 2, D], F32, name="result_tile", align_bytes=64)
             bank = turn_bank([P, 4, P])
             for t in range(4):
                 nc.tensor.transpose(bank[:, t, :], e_turned[b][:, t, 128 * r : 128 * r + 128], ident[:])
@@ -264,7 +285,7 @@ def tile_sensor_residual_squared_d7_kernel(tc, x, g, a, w1_bytes, w1_scale, w2_b
 
         def subtract_direct(b, r):
             nc.vector.tensor_tensor(
-                out=result[b][:, r, HALF:], in0=scratch[b][:, r, :], in1=y_direct[b, r][:], op=ALU.subtract
+                out=result[b][:, r, HALF:], in0=scratch[b + 1][:, r, :], in1=y_direct[b, r][:], op=ALU.subtract
             )
 
         def store(b, tiles, sensors):
@@ -278,65 +299,91 @@ def tile_sensor_residual_squared_d7_kernel(tc, x, g, a, w1_bytes, w1_scale, w2_b
         pick_scales(0)
         for j in (2, 3):
             lace_w1(1, j, on_scalar=True)
-        turn_x(0)
+        banks = [(b, r, turn_x(b, r)) for b in range(2) for r in range(2)]
         for j in range(4):
             lace_w1(0, j, on_scalar=False)
         for j in (0, 1):
             lace_w1(1, j, on_scalar=False)
-        quantize_w(0, 0)
+        for args in banks:
+            lace_x(*args)
+        banks = [(2, r, turn_x(2, r)) for r in range(2)]
+        for c in range(2):
+            quantize_w(0, c)
+        quantize_x(0)
+        widen(nc.vector.tensor_copy, 1, TURNED)
         pick_scales(1)
-        quantize_w(0, 1)
+        for r in range(2):
+            first_product(0, r)
+        widen(nc.scalar.copy, 1, DIRECT)
+        for args in banks:
+            lace_x(*args)
+        for r in range(2):
+            sort_x(3, r)
+        scale_w2(TURNED)
+        quantize_x(1)
+        turn_w2(TURNED)
+        weigh(0, 0)
+        first_product(1, 0)
+        scale_w2(DIRECT)
+        weigh(0, 1)
+        turn_w2(DIRECT)
+        first_product(1, 1)
+        quantize_x(2)
+        quantize_h(0)
+        for r in range(2):
+            weigh(1, r)
+            quantize_w(1, r)
+        for b in (3, 4):
+            turn_and_lace_x(b)
 
         both, last = slice(0, 2), PAIRS - 1
-        for s in range(-3, PAIRS):
-            if s in (-3, -2):
-                widen(nc.scalar.copy, 1, s + 3)
-            if inside(s):
+        for s in range(PAIRS + 1):
+            turned, direct, ahead = inside(s), inside(s - 1), inside(s + 2)
+            if turned:
                 for i in range(2):
                     product_turned(s, i)
             if inside(s + 3):
                 quantize_x(s + 3)
             if inside(s + 1):
                 quantize_h(s + 1)
-                standardise(s + 1)
-            if s in (-3, -2):
-                scale_w2(s + 3)
-            if inside(s + 2):
-                for r in range(2):
-                    first_product(s + 2, r)
-            if inside(s):
-                product_direct(s, 0)
+            elif turned:
+                new_scratch(s + 1)
+            if turned:
+                standardise(s)
+            if direct:
+                product_direct(s - 1, 0)
+            if ahead:
+                first_product(s + 2, 0)
+            if turned:
                 subtract_turned(s, 0)
-                product_direct(s, 1)
+            if ahead:
+                first_product(s + 2, 1)
+            if turned:
                 subtract_turned(s, 1)
-            if inside(s + 2):
+            if direct:
+                product_direct(s - 1, 1)
+                subtract_direct(s - 1, 0)
+            if ahead:
                 for r in range(2):
                     weigh(s + 2, r)
-            if s == -1:
-                for c in range(2):
-                    quantize_w(1, c)
-            if inside(s):
-                for r in range(2):
-                    subtract_direct(s, r)
-            if inside(s + 4):
-                turn_x(s + 4)
-            if s == -2:
-                for c in range(2):
-                    turn_w2(c)
-            if inside(s) and s < last:
+            if direct:
+                subtract_direct(s - 1, 1)
+            if turned:
                 for r in range(2):
                     turn_back(s, r)
                 store(s, both, slice(0, HALF))
-                tile = result[s][:, :, HALF:]
+            if inside(s + 5):
+                turn_and_lace_x(s + 5)
+            if direct and s - 1 < last:
+                tile = result[s - 1][:, :, HALF:]
                 nc.scalar.activation(out=tile, in_=tile, func=ACT.Square)
-                store(s, both, slice(HALF, D))
+                store(s - 1, both, slice(HALF, D))
+            if SORTED_FROM <= s + 6 < PAIRS:
+                sort_x(s + 6, 0)
 
-        for r in range(2):
-            turn_back(last, r)
-            store(last, r, slice(0, HALF))
         tile = result[last][:, 0, HALF:]
-        nc.vector.tensor_tensor(out=tile, in0=tile, in1=tile, op=ALU.mult)
+        nc.scalar.activation(out=tile, in_=tile, func=ACT.Square)
         store(last, 0, slice(HALF, D))
         tile = result[last][:, 1, HALF:]
-        nc.scalar.activation(out=tile, in_=tile, func=ACT.Square)
+        nc.vector.tensor_tensor(out=tile, in0=tile, in1=tile, op=ALU.mult)
         store(last, 1, slice(HALF, D))

@@ -20,7 +20,6 @@ HALF = 512
 PAIRS = T // 256
 TURNED, DIRECT = 0, 1
 MX_BANKS, TURN_BANKS = 4, 4
-SORTED_FROM = 6
 
 
 def tile_sensor_residual_squared_d7_kernel(tc, x, g, a, w1_bytes, w1_scale, w2_bytes, w2_scale, out):
@@ -34,9 +33,9 @@ def tile_sensor_residual_squared_d7_kernel(tc, x, g, a, w1_bytes, w1_scale, w2_b
         psum = ctx.enter_context(tc.psum_pool(name="psum", bufs=1))
         ctx.enter_context(tc.manual_schedule())
 
-        x_raw, x_sorted, x_laced, x_codes, x_scales = {}, {}, {}, {}, {}
-        h_sums, scratch, h_codes, h_scales = {}, {}, {}, {}
-        y_turned, y_direct, e_turned, result = {}, {}, {}, {}
+        x_raw, x_sorted, pair_tile, x_codes, x_scales = {}, {}, {}, {}, {}
+        h_sums, h_tile, h_codes, h_scales = {}, {}, {}, {}
+        xg, y_turned, y_direct, e_turned, result = {}, {}, {}, {}, {}
 
         def mx_bank(shape):
             return psum.tile(shape, F32, name="mx_bank", bufs=MX_BANKS)
@@ -49,23 +48,32 @@ def tile_sensor_residual_squared_d7_kernel(tc, x, g, a, w1_bytes, w1_scale, w2_b
             nc.sync.dma_start(out=tile[:].rearrange("p r d -> p (r d)"), in_=x_pairs[b])
             x_raw[b] = tile
 
-        scales_all = [keep.tile([P, 32], F32, name="scales_all", bufs=2) for w in range(2)]
-        w_raw = {(w, c): keep.tile([P, 4 * R], U8, name="w_raw", align_bytes=64, bufs=4) for w in range(2) for c in range(2)}
-        w_rows = [bytes_in.rearrange("(c p t) n -> p c (t n)", p=P, t=4) for bytes_in in (w1_bytes, w2_bytes)]
+        w_raw = {(w, c): keep.tile([P, 4, R], U8, name="w_raw", align_bytes=64, bufs=4) for w in range(2) for c in range(2)}
+        scale_cols = [keep.tile([P, 2, 4], F32, name="scale_cols", bufs=2) for w in range(2)]
         a_cols = keep.tile([P, 4], BF16, name="a_cols")
         g_cols = keep.tile([P, 4], BF16, name="g_cols")
         g_rows = keep.tile([P, HALF], BF16, name="g_rows", align_bytes=64)
 
-        nc.scalar.dma_start(out=scales_all[0][:], in_=w1_scale.rearrange("i j -> (i j)").partition_broadcast(P))
+        def load_w(w, c):
+            rows = (w1_bytes, w2_bytes)[w].rearrange("(c p t) n -> c p (t n)", p=P, t=4)
+            nc.sync.dma_start(out=w_raw[w, c][:].rearrange("p t n -> p (t n)"), in_=rows[c])
+
+        def load_scales(queue, w):
+            block_rows = (w1_scale, w2_scale)[w].rearrange("(c q) j -> q c j", q=4)
+            for q in range(4):
+                queue.dma_start(out=scale_cols[w][32 * q : 32 * q + 32], in_=block_rows[q].partition_broadcast(32))
+
+        load_scales(nc.scalar, 0)
         for c in range(2):
-            nc.sync.dma_start(out=w_raw[0, c][:], in_=w_rows[0][:, c, :])
-        nc.scalar.dma_start(out=scales_all[1][:], in_=w2_scale.rearrange("i j -> (i j)").partition_broadcast(P))
-        for b in range(3):
+            load_w(0, c)
+        for b in range(2):
             load_x(b)
-        nc.sync.dma_start(out=w_raw[1, 0][:], in_=w_rows[1][:, 0, :])
+        load_scales(nc.sync, 1)
+        for c in range(2):
+            load_w(1, c)
         nc.sync.dma_start(out=a_cols[:], in_=a.rearrange("(p t) -> p t", t=4))
-        nc.sync.dma_start(out=w_raw[1, 1][:], in_=w_rows[1][:, 1, :])
-        load_x(3)
+        for b in range(2, 4):
+            load_x(b)
         nc.sync.dma_start(out=g_rows[:], in_=g[HALF:].partition_broadcast(P))
         nc.sync.dma_start(out=g_cols[:], in_=g[0:HALF].rearrange("(p t) -> p t", t=4))
         for b in range(4, PAIRS):
@@ -74,31 +82,23 @@ def tile_sensor_residual_squared_d7_kernel(tc, x, g, a, w1_bytes, w1_scale, w2_b
         ident = keep.tile([P, P], F32, name="ident", align_bytes=64)
         make_identity(nc, ident[:])
 
-        scale_cols = [keep.tile([P, 2, 4], F32, name="scale_cols", bufs=2) for w in range(2)]
-        wide, laced, w2_scaled = {}, {}, {}
+        w1_wide = [keep.tile([P, 4, R], BF16, name="w1_wide", align_bytes=64, bufs=2) for c in range(2)]
+        w2_scaled = [keep.tile([P, 4, R], BF16, name="w2_scaled", align_bytes=64, bufs=2) for c in range(2)]
+        laced = {(w, c): keep.tile([P, R, 4], BF16, name="laced", align_bytes=64, bufs=4) for w in range(2) for c in range(2)}
         w_codes = [keep.tile([P, 2, R], U32, name="w_codes", align_bytes=64, bufs=2) for w in range(2)]
         w_scales = [keep.tile([P, 2, R], U8, name="w_scales", align_bytes=64, bufs=2) for w in range(2)]
+        w2_banks = {}
 
-        def pick_scales(w):
-            for q in range(4):
-                quadrant = slice(32 * q, 32 * q + 32)
-                nc.vector.tensor_copy(
-                    out=scale_cols[w][quadrant],
-                    in_=scales_all[w][quadrant].rearrange("p (c q j) -> p c q j", q=4, j=4)[:, :, q, :],
-                )
-
-        def widen(copy, w, c):
-            wide[w, c] = keep.tile([P, 4, R], BF16, name="wide", align_bytes=64, bufs=4)
-            copy(out=wide[w, c][:].rearrange("p t n -> p (t n)"), in_=w_raw[w, c][:].bitcast(E4M3))
-
-        def laced_of(w, c):
-            if (w, c) not in laced:
-                laced[w, c] = keep.tile([P, R, 4], BF16, name="laced", align_bytes=64, bufs=4)
-            return laced[w, c]
+        def widen_w1():
+            raw = [w_raw[0, c][:].rearrange("p t n -> p (t n)").bitcast(E4M3) for c in range(2)]
+            wide = [w1_wide[c][:].rearrange("p t n -> p (t n)") for c in range(2)]
+            nc.vector.tensor_copy(out=wide[0], in_=raw[0])
+            nc.scalar.activation(out=wide[1][:, 0:P], in_=raw[1][:, 0:P], func=ACT.Copy)
+            nc.scalar.copy(out=wide[1][:, P:], in_=raw[1][:, P:])
 
         def lace_w1(c, j, on_scalar):
-            out_ = laced_of(0, c)[:].rearrange("p (u m) t -> p u m t", u=4)[:, :, 32 * j : 32 * j + 32, :]
-            in_ = wide[0, c][:, :, 128 * j : 128 * j + 128].rearrange("p t (m u) -> p u m t", u=4)
+            out_ = laced[0, c][:].rearrange("p (u m) t -> p u m t", u=4)[:, :, 32 * j : 32 * j + 32, :]
+            in_ = w1_wide[c][:, :, 128 * j : 128 * j + 128].rearrange("p t (m u) -> p u m t", u=4)
             scale = scale_cols[0][:, c, j : j + 1]
             if on_scalar:
                 nc.scalar.activation(out=out_, in_=in_, func=ACT.Copy, scale=scale)
@@ -106,35 +106,41 @@ def tile_sensor_residual_squared_d7_kernel(tc, x, g, a, w1_bytes, w1_scale, w2_b
                 nc.vector.tensor_scalar(out=out_, in0=in_, scalar1=scale, scalar2=None, op0=ALU.mult)
 
         def scale_w2(c):
-            w2_scaled[c] = keep.tile([P, 4, R], BF16, name="w2_scaled", align_bytes=64, bufs=2)
-            for j in range(4):
-                columns = slice(128 * j, 128 * j + 128)
-                nc.vector.tensor_scalar(
-                    out=w2_scaled[c][:, :, columns],
-                    in0=wide[1, c][:, :, columns],
-                    scalar1=scale_cols[1][:, c, j : j + 1],
-                    scalar2=None,
-                    op0=ALU.mult,
-                )
+            for t in range(4):
+                for j in range(4):
+                    columns = slice(128 * j, 128 * j + 128)
+                    in_ = w_raw[1, c][:, t, columns].bitcast(E4M3)
+                    scale = scale_cols[1][:, c, j : j + 1]
+                    if c == TURNED:
+                        by_word = w2_scaled[c][:, t, :].rearrange("p (u m e) -> p m u e", u=2, e=2)
+                        nc.vector.tensor_scalar(
+                            out=by_word[:, 32 * j : 32 * j + 32],
+                            in0=in_.rearrange("p (m u e) -> p m u e", u=2, e=2),
+                            scalar1=scale,
+                            scalar2=None,
+                            op0=ALU.mult,
+                        )
+                    else:
+                        nc.scalar.activation(out=w2_scaled[c][:, t, columns], in_=in_, func=ACT.Copy, scale=scale)
 
         def turn_w2(c):
-            words_out = laced_of(1, c)[:].bitcast(F32)
             for i in range(2):
                 bank = turn_bank([P, 2, 2, P])
                 for k in range(2):
                     words = w2_scaled[c][:, 2 * i + k, :].bitcast(F32)
                     for u in range(2):
-                        nc.tensor.transpose(bank[:, k, u, :], words[:, u::2], ident[:])
-                if c == TURNED:
-                    nc.scalar.copy(
-                        out=words_out.rearrange("p (t m) u -> p t m u", t=4)[:, 2 * i : 2 * i + 2],
-                        in_=bank[:].rearrange("p k u m -> p k m u"),
-                    )
-                else:
-                    nc.scalar.copy(
-                        out=words_out.rearrange("p (m t) u -> p m t u", t=4)[:, :, 2 * i : 2 * i + 2, :],
-                        in_=bank[:].rearrange("p k u m -> p m k u"),
-                    )
+                        source = words[:, P * u : P * u + P] if c == TURNED else words[:, u::2]
+                        nc.tensor.transpose(bank[:, k, u, :], source, ident[:])
+                w2_banks[c, i] = bank
+
+        def lace_w2(c, i, copy):
+            words, bank = laced[1, c][:].bitcast(F32), w2_banks[c, i]
+            if c == TURNED:
+                out_ = words.rearrange("p (t m) u -> p t m u", t=4)[:, 2 * i : 2 * i + 2]
+                copy(out=out_, in_=bank[:].rearrange("p k u m -> p k m u"))
+            else:
+                out_ = words.rearrange("p (m t) u -> p m t u", t=4)[:, :, 2 * i : 2 * i + 2, :]
+                copy(out=out_, in_=bank[:].rearrange("p k u m -> p m k u"))
 
         def quantize_w(w, c):
             nc.vector.quantize_mx(
@@ -161,11 +167,14 @@ def tile_sensor_residual_squared_d7_kernel(tc, x, g, a, w1_bytes, w1_scale, w2_b
                     nc.tensor.transpose(bank[:, c, u, :], source, ident[:])
             return bank
 
+        def x_laced(b):
+            return pair_tile[b][:, 0:2, :].bitcast(BF16).rearrange("p c (n t) -> p c n t", t=4)
+
         def lace_x(b, r, bank):
             if r == 0:
-                x_laced[b] = work.tile([P, 2, 256, 4], BF16, name="x_laced_tile", align_bytes=64, bufs=7)
+                pair_tile[b] = work.tile([P, 3, HALF], F32, name="pair_tile", align_bytes=64, bufs=5)
             nc.scalar.copy(
-                out=x_laced[b][:, :, 128 * r : 128 * r + 128, :].bitcast(F32),
+                out=x_laced(b)[:, :, 128 * r : 128 * r + 128, :].bitcast(F32),
                 in_=bank[:].rearrange("p c u n -> p c n u"),
             )
 
@@ -179,7 +188,7 @@ def tile_sensor_residual_squared_d7_kernel(tc, x, g, a, w1_bytes, w1_scale, w2_b
             nc.vector.quantize_mx(
                 out=x_codes[b][:].rearrange("p c n -> p (c n)").bitcast(X4),
                 scales=x_scales[b][:].rearrange("p c n -> p (c n)"),
-                in_=x_laced[b][:].rearrange("p c n t -> p (c n t)"),
+                in_=x_laced(b).rearrange("p c n t -> p (c n t)"),
             )
 
         def first_product(b, r):
@@ -199,15 +208,12 @@ def tile_sensor_residual_squared_d7_kernel(tc, x, g, a, w1_bytes, w1_scale, w2_b
                     )
             h_sums[b, r] = bank
 
-        def new_scratch(b):
-            scratch[b] = work.tile([P, 2, HALF], F32, name="scratch_tile", align_bytes=64, bufs=4)
-
         def h_laced(b):
-            return scratch[b][:, 0, :].bitcast(BF16)
+            return h_tile[b][:, 0, :].bitcast(BF16)
 
         def weigh(b, r):
             if r == 0:
-                new_scratch(b)
+                h_tile[b] = work.tile([P, 2, HALF], F32, name="h_tile", align_bytes=64, bufs=2)
             nc.vector.tensor_tensor(
                 out=h_laced(b).rearrange("p (r n t) -> p r n t", r=2, t=4)[:, r],
                 in0=h_sums[b, r][:].rearrange("p u n -> p n u"),
@@ -216,17 +222,28 @@ def tile_sensor_residual_squared_d7_kernel(tc, x, g, a, w1_bytes, w1_scale, w2_b
             )
 
         def quantize_h(b):
-            h_codes[b] = work.tile([P, 256], U32, name="h_codes_tile", align_bytes=64, bufs=4)
-            h_scales[b] = work.tile([P, 256], U8, name="h_scales_tile", align_bytes=64, bufs=4)
+            h_codes[b] = work.tile([P, 256], U32, name="h_codes_tile", align_bytes=64)
+            h_scales[b] = work.tile([P, 256], U8, name="h_scales_tile", align_bytes=64)
             nc.vector.quantize_mx(out=h_codes[b][:].bitcast(X4), scales=h_scales[b][:], in_=h_laced(b))
 
         def standardise(b):
+            if b == 0:
+                xg[b] = laced[1, DIRECT][:].rearrange("p (r n) t -> p r (n t)", r=2).bitcast(F32)
+            elif inside(b + 1):
+                xg[b] = pair_tile[b + 1][:, 1:3, :]
+            else:
+                xg[b] = h_tile[b][:]
             nc.gpsimd.tensor_tensor(
-                out=scratch[b + 1][:],
+                out=xg[b],
                 in0=x_raw[b][:, :, HALF:],
                 in1=g_rows[:].unsqueeze(1).to_broadcast([P, 2, HALF]),
                 op=ALU.mult,
             )
+
+        def result_of(b):
+            if b not in result:
+                result[b] = work.tile([P, 2, D], F32, name="result_tile", align_bytes=64)
+            return result[b]
 
         def product_turned(b, i):
             bank = mx_bank([P, 2, 256])
@@ -250,7 +267,7 @@ def tile_sensor_residual_squared_d7_kernel(tc, x, g, a, w1_bytes, w1_scale, w2_b
                 t = 2 * i + k
                 nc.vector.scalar_tensor_tensor(
                     out=e_turned[b][:, t, :],
-                    in0=x_laced[b][:, TURNED, :, t],
+                    in0=x_laced(b)[:, TURNED, :, t],
                     scalar=g_cols[:, t : t + 1],
                     in1=y_turned[b, i][:, k, :],
                     op0=ALU.mult,
@@ -258,13 +275,11 @@ def tile_sensor_residual_squared_d7_kernel(tc, x, g, a, w1_bytes, w1_scale, w2_b
                 )
 
         def turn_back(b, r):
-            if r == 0:
-                result[b] = work.tile([P, 2, D], F32, name="result_tile", align_bytes=64)
             bank = turn_bank([P, 4, P])
             for t in range(4):
                 nc.tensor.transpose(bank[:, t, :], e_turned[b][:, t, 128 * r : 128 * r + 128], ident[:])
             nc.scalar.activation(
-                out=result[b][:, r, 0:HALF].rearrange("p (m t) -> p m t", t=4),
+                out=result_of(b)[:, r, 0:HALF].rearrange("p (m t) -> p m t", t=4),
                 in_=bank[:].rearrange("p t m -> p m t"),
                 func=ACT.Square,
             )
@@ -285,18 +300,23 @@ def tile_sensor_residual_squared_d7_kernel(tc, x, g, a, w1_bytes, w1_scale, w2_b
 
         def subtract_direct(b, r):
             nc.vector.tensor_tensor(
-                out=result[b][:, r, HALF:], in0=scratch[b + 1][:, r, :], in1=y_direct[b, r][:], op=ALU.subtract
+                out=result_of(b)[:, r, HALF:], in0=xg[b][:, r, :], in1=y_direct[b, r][:], op=ALU.subtract
             )
 
-        def store(b, tiles, sensors):
-            nc.sync.dma_start(out=out_pairs[b][:, tiles, sensors], in_=result[b][:, tiles, sensors])
+        def square_direct(b, r):
+            tile = result[b][:, r, HALF:]
+            if b < PAIRS - 1:
+                nc.scalar.activation(out=tile, in_=tile, func=ACT.Square)
+            else:
+                nc.vector.tensor_tensor(out=tile, in0=tile, in1=tile, op=ALU.mult)
+
+        def store(b, r, sensors):
+            nc.sync.dma_start(out=out_pairs[b][:, r, sensors], in_=result[b][:, r, sensors])
 
         def inside(b):
             return 0 <= b < PAIRS
 
-        widen(nc.vector.tensor_copy, 0, 0)
-        widen(nc.scalar.copy, 0, 1)
-        pick_scales(0)
+        widen_w1()
         for j in (2, 3):
             lace_w1(1, j, on_scalar=True)
         banks = [(b, r, turn_x(b, r)) for b in range(2) for r in range(2)]
@@ -306,84 +326,72 @@ def tile_sensor_residual_squared_d7_kernel(tc, x, g, a, w1_bytes, w1_scale, w2_b
             lace_w1(1, j, on_scalar=False)
         for args in banks:
             lace_x(*args)
-        banks = [(2, r, turn_x(2, r)) for r in range(2)]
         for c in range(2):
             quantize_w(0, c)
         quantize_x(0)
-        widen(nc.vector.tensor_copy, 1, TURNED)
-        pick_scales(1)
-        for r in range(2):
-            first_product(0, r)
-        widen(nc.scalar.copy, 1, DIRECT)
-        for args in banks:
-            lace_x(*args)
-        for r in range(2):
-            sort_x(3, r)
-        scale_w2(TURNED)
-        quantize_x(1)
+        for c in range(2):
+            scale_w2(c)
+        first_product(0, 0)
         turn_w2(TURNED)
+        first_product(0, 1)
+        quantize_x(1)
         weigh(0, 0)
-        first_product(1, 0)
-        scale_w2(DIRECT)
+        lace_w2(TURNED, 0, nc.vector.tensor_copy)
+        lace_w2(TURNED, 1, nc.scalar.copy)
         weigh(0, 1)
         turn_w2(DIRECT)
-        first_product(1, 1)
-        quantize_x(2)
+        quantize_w(1, TURNED)
         quantize_h(0)
-        for r in range(2):
-            weigh(1, r)
-            quantize_w(1, r)
-        for b in (3, 4):
-            turn_and_lace_x(b)
+        for i in range(2):
+            lace_w2(DIRECT, i, nc.scalar.copy)
+        turn_and_lace_x(2)
+        quantize_w(1, DIRECT)
+        standardise(0)
+        sort_x(3, 0)
 
-        both, last = slice(0, 2), PAIRS - 1
-        for s in range(PAIRS + 1):
-            turned, direct, ahead = inside(s), inside(s - 1), inside(s + 2)
-            if turned:
-                for i in range(2):
-                    product_turned(s, i)
-            if inside(s + 3):
-                quantize_x(s + 3)
-            if inside(s + 1):
-                quantize_h(s + 1)
-            elif turned:
-                new_scratch(s + 1)
-            if turned:
-                standardise(s)
-            if direct:
-                product_direct(s - 1, 0)
-            if ahead:
-                first_product(s + 2, 0)
-            if turned:
-                subtract_turned(s, 0)
-            if ahead:
-                first_product(s + 2, 1)
-            if turned:
-                subtract_turned(s, 1)
-            if direct:
+        whole, last = slice(0, D), PAIRS - 1
+        for s in range(PAIRS):
+            if s > 0:
                 product_direct(s - 1, 1)
-                subtract_direct(s - 1, 0)
-            if ahead:
-                for r in range(2):
-                    weigh(s + 2, r)
-            if direct:
+            for i in range(2):
+                product_turned(s, i)
+            if s < last:
+                first_product(s + 1, 0)
+            else:
+                product_direct(s, 0)
+            if s > 0:
                 subtract_direct(s - 1, 1)
-            if turned:
+                square_direct(s - 1, 1)
+                store(s - 1, 1, whole)
+            if s < last:
+                first_product(s + 1, 1)
+            else:
+                product_direct(s, 1)
+            subtract_turned(s, 0)
+            if s < last:
+                product_direct(s, 0)
+            subtract_turned(s, 1)
+            if s < last:
+                for r in range(2):
+                    weigh(s + 1, r)
+            if s > 0 and inside(s + 3):
+                sort_x(s + 3, 1)
+            subtract_direct(s, 0)
+            if s < last:
+                quantize_h(s + 1)
+                if inside(s + 2):
+                    quantize_x(s + 2)
+                standardise(s + 1)
                 for r in range(2):
                     turn_back(s, r)
-                store(s, both, slice(0, HALF))
-            if inside(s + 5):
-                turn_and_lace_x(s + 5)
-            if direct and s - 1 < last:
-                tile = result[s - 1][:, :, HALF:]
-                nc.scalar.activation(out=tile, in_=tile, func=ACT.Square)
-                store(s - 1, both, slice(HALF, D))
-            if SORTED_FROM <= s + 6 < PAIRS:
-                sort_x(s + 6, 0)
+                square_direct(s, 0)
+                store(s, 0, whole)
+            if inside(s + 3):
+                turn_and_lace_x(s + 3)
 
-        tile = result[last][:, 0, HALF:]
-        nc.scalar.activation(out=tile, in_=tile, func=ACT.Square)
-        store(last, 0, slice(HALF, D))
-        tile = result[last][:, 1, HALF:]
-        nc.vector.tensor_tensor(out=tile, in0=tile, in1=tile, op=ALU.mult)
-        store(last, 1, slice(HALF, D))
+        subtract_direct(last, 1)
+        for r in range(2):
+            turn_back(last, r)
+            store(last, r, slice(0, HALF))
+            square_direct(last, r)
+            store(last, r, slice(HALF, D))

@@ -208,14 +208,11 @@ def tile_sensor_residual_squared_d7_kernel(tc, x, g, a, w1_bytes, w1_scale, w2_b
                     )
             h_sums[b, r] = bank
 
-        def h_laced(b):
-            return h_tile[b][:, 0, :].bitcast(BF16)
-
         def weigh(b, r):
             if r == 0:
-                h_tile[b] = work.tile([P, 2, HALF], F32, name="h_tile", align_bytes=64, bufs=2)
+                h_tile[b] = work.tile([P, 2, P, 4], BF16, name="h_tile", align_bytes=64, bufs=2)
             nc.vector.tensor_tensor(
-                out=h_laced(b).rearrange("p (r n t) -> p r n t", r=2, t=4)[:, r],
+                out=h_tile[b][:, r],
                 in0=h_sums[b, r][:].rearrange("p u n -> p n u"),
                 in1=a_cols[:].unsqueeze(1).to_broadcast([P, P, 4]),
                 op=ALU.mult,
@@ -224,16 +221,18 @@ def tile_sensor_residual_squared_d7_kernel(tc, x, g, a, w1_bytes, w1_scale, w2_b
         def quantize_h(b):
             h_codes[b] = work.tile([P, 256], U32, name="h_codes_tile", align_bytes=64)
             h_scales[b] = work.tile([P, 256], U8, name="h_scales_tile", align_bytes=64)
-            nc.vector.quantize_mx(out=h_codes[b][:].bitcast(X4), scales=h_scales[b][:], in_=h_laced(b))
+            nc.vector.quantize_mx(
+                out=h_codes[b][:].bitcast(X4),
+                scales=h_scales[b][:],
+                in_=h_tile[b][:].rearrange("p r n t -> p (r n t)"),
+            )
 
-        def standardise(b):
-            if b == 0:
+        def standardise(b, engine):
+            if b == 1:
                 xg[b] = laced[1, DIRECT][:].rearrange("p (r n) t -> p r (n t)", r=2).bitcast(F32)
-            elif inside(b + 1):
-                xg[b] = pair_tile[b + 1][:, 1:3, :]
             else:
-                xg[b] = h_tile[b][:]
-            nc.gpsimd.tensor_tensor(
+                xg[b] = pair_tile[b][:, 1:3, :]
+            engine.tensor_tensor(
                 out=xg[b],
                 in0=x_raw[b][:, :, HALF:],
                 in1=g_rows[:].unsqueeze(1).to_broadcast([P, 2, HALF]),
@@ -342,11 +341,12 @@ def tile_sensor_residual_squared_d7_kernel(tc, x, g, a, w1_bytes, w1_scale, w2_b
         turn_w2(DIRECT)
         quantize_w(1, TURNED)
         quantize_h(0)
+        standardise(0, nc.vector)
         for i in range(2):
             lace_w2(DIRECT, i, nc.scalar.copy)
         turn_and_lace_x(2)
         quantize_w(1, DIRECT)
-        standardise(0)
+        standardise(1, nc.gpsimd)
         sort_x(3, 0)
 
         whole, last = slice(0, D), PAIRS - 1
@@ -381,7 +381,7 @@ def tile_sensor_residual_squared_d7_kernel(tc, x, g, a, w1_bytes, w1_scale, w2_b
                 quantize_h(s + 1)
                 if inside(s + 2):
                     quantize_x(s + 2)
-                standardise(s + 1)
+                    standardise(s + 2, nc.gpsimd)
                 for r in range(2):
                     turn_back(s, r)
                 square_direct(s, 0)

@@ -37,6 +37,8 @@ def tile_sensor_residual_squared_d7_kernel(tc, x, g, a, w1_bytes, w1_scale, w2_b
         h_sums, h_tile, h_codes, h_scales = {}, {}, {}, {}
         xg, y_turned, y_direct, e_turned, result = {}, {}, {}, {}, {}
 
+        is_sorted = set()
+
         def mx_bank(shape):
             return psum.tile(shape, F32, name="mx_bank", bufs=MX_BANKS)
 
@@ -149,19 +151,21 @@ def tile_sensor_residual_squared_d7_kernel(tc, x, g, a, w1_bytes, w1_scale, w2_b
                 in_=laced[w, c][:].rearrange("p n t -> p (n t)"),
             )
 
-        def sort_x(b, r):
-            tile = work.tile([P, 2, 2, P], F32, name="x_sorted_tile", align_bytes=64)
-            words = x_raw[b][:, r, :].bitcast(F32)
-            nc.scalar.copy(out=tile[:], in_=words.rearrange("p (c m u) -> p c u m", c=2, u=2))
-            x_sorted[b, r] = tile
+        def sort_x(b, r, passes, copy):
+            if b not in x_sorted:
+                x_sorted[b] = work.tile([P, 2, 2, 2, P], U32, name="x_sorted_tile", align_bytes=64, bufs=4)
+            words = x_raw[b][:, r, :].bitcast(U32).rearrange("p (c m u) -> p c u m", c=2, u=2)
+            copy(out=x_sorted[b][:, r, passes], in_=words[:, passes])
+            for c in range(passes.start, passes.stop):
+                is_sorted.add((b, r, c))
 
         def turn_x(b, r):
             bank = turn_bank([P, 2, 2, P])
             words = x_raw[b][:, r, :].bitcast(F32)
             for c in range(2):
                 for u in range(2):
-                    if (b, r) in x_sorted:
-                        source = x_sorted[b, r][:, c, u, :]
+                    if (b, r, c) in is_sorted:
+                        source = x_sorted[b][:, r, c, u, :].bitcast(F32)
                     else:
                         source = words[:, 256 * c + u : 256 * (c + 1) : 2]
                     nc.tensor.transpose(bank[:, c, u, :], source, ident[:])
@@ -347,7 +351,7 @@ def tile_sensor_residual_squared_d7_kernel(tc, x, g, a, w1_bytes, w1_scale, w2_b
         turn_and_lace_x(2)
         quantize_w(1, DIRECT)
         standardise(1, nc.gpsimd)
-        sort_x(3, 0)
+        sort_x(3, 0, slice(0, 2), nc.scalar.copy)
 
         whole, last = slice(0, D), PAIRS - 1
         for s in range(PAIRS):
@@ -375,13 +379,15 @@ def tile_sensor_residual_squared_d7_kernel(tc, x, g, a, w1_bytes, w1_scale, w2_b
                 for r in range(2):
                     weigh(s + 1, r)
             if s > 0 and inside(s + 3):
-                sort_x(s + 3, 1)
+                sort_x(s + 3, 1, slice(0, 2), nc.scalar.copy)
             subtract_direct(s, 0)
             if s < last:
                 quantize_h(s + 1)
                 if inside(s + 2):
                     quantize_x(s + 2)
                     standardise(s + 2, nc.gpsimd)
+                if inside(s + 5):
+                    sort_x(s + 5, 0, slice(0, 1), nc.gpsimd.tensor_copy)
                 for r in range(2):
                     turn_back(s, r)
                 square_direct(s, 0)

@@ -74,9 +74,9 @@ def tile_sensor_residual_squared_d7_kernel(tc, x, g, a, w1_bytes, w1_scale, w2_b
         for c in range(2):
             load_w(1, c)
         nc.sync.dma_start(out=a_cols[:], in_=a.rearrange("(p t) -> p t", t=4))
+        nc.sync.dma_start(out=g_rows[:], in_=g[HALF:].partition_broadcast(P))
         for b in range(2, 4):
             load_x(b)
-        nc.sync.dma_start(out=g_rows[:], in_=g[HALF:].partition_broadcast(P))
         nc.sync.dma_start(out=g_cols[:], in_=g[0:HALF].rearrange("(p t) -> p t", t=4))
         for b in range(4, PAIRS):
             load_x(b)
@@ -111,19 +111,12 @@ def tile_sensor_residual_squared_d7_kernel(tc, x, g, a, w1_bytes, w1_scale, w2_b
             for t in range(4):
                 for j in range(4):
                     columns = slice(128 * j, 128 * j + 128)
-                    in_ = w_raw[1, c][:, t, columns].bitcast(E4M3)
+                    out_, in_ = w2_scaled[c][:, t, columns], w_raw[1, c][:, t, columns].bitcast(E4M3)
                     scale = scale_cols[1][:, c, j : j + 1]
                     if c == TURNED:
-                        by_word = w2_scaled[c][:, t, :].rearrange("p (u m e) -> p m u e", u=2, e=2)
-                        nc.vector.tensor_scalar(
-                            out=by_word[:, 32 * j : 32 * j + 32],
-                            in0=in_.rearrange("p (m u e) -> p m u e", u=2, e=2),
-                            scalar1=scale,
-                            scalar2=None,
-                            op0=ALU.mult,
-                        )
+                        nc.vector.tensor_scalar(out=out_, in0=in_, scalar1=scale, scalar2=None, op0=ALU.mult)
                     else:
-                        nc.scalar.activation(out=w2_scaled[c][:, t, columns], in_=in_, func=ACT.Copy, scale=scale)
+                        nc.scalar.activation(out=out_, in_=in_, func=ACT.Copy, scale=scale)
 
         def turn_w2(c):
             for i in range(2):
@@ -131,8 +124,7 @@ def tile_sensor_residual_squared_d7_kernel(tc, x, g, a, w1_bytes, w1_scale, w2_b
                 for k in range(2):
                     words = w2_scaled[c][:, 2 * i + k, :].bitcast(F32)
                     for u in range(2):
-                        source = words[:, P * u : P * u + P] if c == TURNED else words[:, u::2]
-                        nc.tensor.transpose(bank[:, k, u, :], source, ident[:])
+                        nc.tensor.transpose(bank[:, k, u, :], words[:, u::2], ident[:])
                 w2_banks[c, i] = bank
 
         def lace_w2(c, i, copy):
@@ -231,22 +223,38 @@ def tile_sensor_residual_squared_d7_kernel(tc, x, g, a, w1_bytes, w1_scale, w2_b
                 in_=h_tile[b][:].rearrange("p r n t -> p (r n t)"),
             )
 
-        def standardise(b, engine):
+        def standardise(b):
             if b == 1:
                 xg[b] = laced[1, DIRECT][:].rearrange("p (r n) t -> p r (n t)", r=2).bitcast(F32)
             else:
                 xg[b] = pair_tile[b][:, 1:3, :]
-            engine.tensor_tensor(
+            nc.gpsimd.tensor_tensor(
                 out=xg[b],
                 in0=x_raw[b][:, :, HALF:],
                 in1=g_rows[:].unsqueeze(1).to_broadcast([P, 2, HALF]),
                 op=ALU.mult,
             )
 
+        first_xg = {}
+
+        def standardise_first(r, engine, home):
+            first_xg[r] = home
+            engine.tensor_tensor(out=home, in0=x_raw[0][:, r, HALF:], in1=g_rows[:], op=ALU.mult)
+
         def result_of(b):
             if b not in result:
                 result[b] = work.tile([P, 2, D], F32, name="result_tile", align_bytes=64)
             return result[b]
+
+        def on_tensor(b):
+            return not inside(b + 3)
+
+        g_first = keep.tile([P, 1], F32, name="g_first")
+        g_diag = keep.tile([P, P], BF16, name="g_diag", align_bytes=64)
+
+        def make_g_diag():
+            nc.scalar.activation(out=g_first[:], in_=g_cols[:, 0:1], func=ACT.Copy)
+            nc.scalar.activation(out=g_diag[:], in_=ident[:], func=ACT.Copy, scale=g_first[:])
 
         def product_turned(b, i):
             bank = mx_bank([P, 2, 256])
@@ -268,6 +276,8 @@ def tile_sensor_residual_squared_d7_kernel(tc, x, g, a, w1_bytes, w1_scale, w2_b
                 e_turned[b] = work.tile([P, 4, 256], F32, name="e_turned_tile", align_bytes=64, bufs=2)
             for k in range(2):
                 t = 2 * i + k
+                if t == 0 and on_tensor(b):
+                    continue
                 nc.vector.scalar_tensor_tensor(
                     out=e_turned[b][:, t, :],
                     in0=x_laced(b)[:, TURNED, :, t],
@@ -277,10 +287,26 @@ def tile_sensor_residual_squared_d7_kernel(tc, x, g, a, w1_bytes, w1_scale, w2_b
                     op1=ALU.subtract,
                 )
 
+        def negate_first(b):
+            nc.scalar.activation(out=e_turned[b][:, 0, :], in_=y_turned[b, 0][:, 0, :], func=ACT.Copy, scale=-1.0)
+
+        back_banks = {}
+
+        def open_back(b):
+            for r in range(2):
+                back_banks[b, r] = turn_bank([P, 4, P])
+                if on_tensor(b):
+                    x_first = x_laced(b)[:, TURNED, 128 * r : 128 * r + 128, 0]
+                    nc.tensor.matmul(back_banks[b, r][:, 0, :], x_first, g_diag[:], start=True, stop=False)
+
         def turn_back(b, r):
-            bank = turn_bank([P, 4, P])
+            bank = back_banks[b, r]
             for t in range(4):
-                nc.tensor.transpose(bank[:, t, :], e_turned[b][:, t, 128 * r : 128 * r + 128], ident[:])
+                source = e_turned[b][:, t, 128 * r : 128 * r + 128]
+                if t == 0 and on_tensor(b):
+                    nc.tensor.matmul(bank[:, t, :], source, ident[:], start=False, stop=True, is_transpose=True)
+                else:
+                    nc.tensor.transpose(bank[:, t, :], source, ident[:])
             nc.scalar.activation(
                 out=result_of(b)[:, r, 0:HALF].rearrange("p (m t) -> p m t", t=4),
                 in_=bank[:].rearrange("p t m -> p m t"),
@@ -303,7 +329,7 @@ def tile_sensor_residual_squared_d7_kernel(tc, x, g, a, w1_bytes, w1_scale, w2_b
 
         def subtract_direct(b, r):
             nc.vector.tensor_tensor(
-                out=result_of(b)[:, r, HALF:], in0=xg[b][:, r, :], in1=y_direct[b, r][:], op=ALU.subtract
+                out=result_of(b)[:, r, HALF:], in0=xg[b][:, r, :] if b else first_xg[r], in1=y_direct[b, r][:], op=ALU.subtract
             )
 
         def square_direct(b, r):
@@ -338,6 +364,7 @@ def tile_sensor_residual_squared_d7_kernel(tc, x, g, a, w1_bytes, w1_scale, w2_b
         turn_w2(TURNED)
         first_product(0, 1)
         quantize_x(1)
+        standardise_first(1, nc.gpsimd, pair_tile[1][:, 1, :])
         weigh(0, 0)
         lace_w2(TURNED, 0, nc.vector.tensor_copy)
         lace_w2(TURNED, 1, nc.scalar.copy)
@@ -345,13 +372,14 @@ def tile_sensor_residual_squared_d7_kernel(tc, x, g, a, w1_bytes, w1_scale, w2_b
         turn_w2(DIRECT)
         quantize_w(1, TURNED)
         quantize_h(0)
-        standardise(0, nc.vector)
+        standardise_first(0, nc.vector, pair_tile[0][:, 1, :])
         for i in range(2):
             lace_w2(DIRECT, i, nc.scalar.copy)
         turn_and_lace_x(2)
         quantize_w(1, DIRECT)
-        standardise(1, nc.gpsimd)
+        standardise(1)
         sort_x(3, 0, slice(0, 2), nc.scalar.copy)
+        make_g_diag()
 
         whole, last = slice(0, D), PAIRS - 1
         for s in range(PAIRS):
@@ -365,13 +393,16 @@ def tile_sensor_residual_squared_d7_kernel(tc, x, g, a, w1_bytes, w1_scale, w2_b
                 product_direct(s, 0)
             if s > 0:
                 subtract_direct(s - 1, 1)
-                square_direct(s - 1, 1)
-                store(s - 1, 1, whole)
             if s < last:
                 first_product(s + 1, 1)
             else:
                 product_direct(s, 1)
             subtract_turned(s, 0)
+            if on_tensor(s):
+                negate_first(s)
+            if s > 0:
+                square_direct(s - 1, 1)
+                store(s - 1, 1, whole)
             if s < last:
                 product_direct(s, 0)
             subtract_turned(s, 1)
@@ -385,9 +416,10 @@ def tile_sensor_residual_squared_d7_kernel(tc, x, g, a, w1_bytes, w1_scale, w2_b
                 quantize_h(s + 1)
                 if inside(s + 2):
                     quantize_x(s + 2)
-                    standardise(s + 2, nc.gpsimd)
+                    standardise(s + 2)
                 if inside(s + 5):
                     sort_x(s + 5, 0, slice(0, 1), nc.gpsimd.tensor_copy)
+                open_back(s)
                 for r in range(2):
                     turn_back(s, r)
                 square_direct(s, 0)
@@ -396,6 +428,7 @@ def tile_sensor_residual_squared_d7_kernel(tc, x, g, a, w1_bytes, w1_scale, w2_b
                 turn_and_lace_x(s + 3)
 
         subtract_direct(last, 1)
+        open_back(last)
         for r in range(2):
             turn_back(last, r)
             store(last, r, slice(0, HALF))

@@ -99,8 +99,8 @@ def tile_sensor_residual_squared_d7_kernel(tc, x, g, a, w1_bytes, w1_scale, w2_b
             nc.scalar.copy(out=wide[1][:, P:], in_=raw[1][:, P:])
 
         def lace_w1(c, j, on_scalar):
-            out_ = laced[0, c][:].rearrange("p (u m) t -> p u m t", u=4)[:, :, 32 * j : 32 * j + 32, :]
-            in_ = w1_wide[c][:, :, 128 * j : 128 * j + 128].rearrange("p t (m u) -> p u m t", u=4)
+            out_ = laced[0, c][:].rearrange("p (u m) t -> p m u t", u=4)[:, 32 * j : 32 * j + 32]
+            in_ = w1_wide[c][:, :, 128 * j : 128 * j + 128].rearrange("p t (m u) -> p m u t", u=4)
             scale = scale_cols[0][:, c, j : j + 1]
             if on_scalar:
                 nc.scalar.activation(out=out_, in_=in_, func=ACT.Copy, scale=scale)
@@ -381,7 +381,7 @@ def tile_sensor_residual_squared_d7_kernel(tc, x, g, a, w1_bytes, w1_scale, w2_b
         sort_x(3, 0, slice(0, 2), nc.scalar.copy)
         make_g_diag()
 
-        whole, last = slice(0, D), PAIRS - 1
+        whole, turned, direct, last = slice(0, D), slice(0, HALF), slice(HALF, D), PAIRS - 1
         for s in range(PAIRS):
             if s > 0:
                 product_direct(s - 1, 1)
@@ -402,7 +402,7 @@ def tile_sensor_residual_squared_d7_kernel(tc, x, g, a, w1_bytes, w1_scale, w2_b
                 negate_first(s)
             if s > 0:
                 square_direct(s - 1, 1)
-                store(s - 1, 1, whole)
+                store(s - 1, 1, whole if s < last else direct)
             if s < last:
                 product_direct(s, 0)
             subtract_turned(s, 1)
@@ -422,15 +422,20 @@ def tile_sensor_residual_squared_d7_kernel(tc, x, g, a, w1_bytes, w1_scale, w2_b
                 open_back(s)
                 for r in range(2):
                     turn_back(s, r)
+                    if s == last - 1:
+                        store(s, r, turned)
                 square_direct(s, 0)
-                store(s, 0, whole)
+                store(s, 0, whole if s < last - 1 else direct)
             if inside(s + 3):
                 turn_and_lace_x(s + 3)
 
-        subtract_direct(last, 1)
         open_back(last)
-        for r in range(2):
-            turn_back(last, r)
-            store(last, r, slice(0, HALF))
-            square_direct(last, r)
-            store(last, r, slice(HALF, D))
+        square_direct(last, 0)
+        store(last, 0, direct)
+        subtract_direct(last, 1)
+        turn_back(last, 0)
+        store(last, 0, turned)
+        turn_back(last, 1)
+        store(last, 1, turned)
+        square_direct(last, 1)
+        store(last, 1, direct)

@@ -146,8 +146,9 @@ def tile_sensor_residual_squared_d7_kernel(tc, x, g, a, w1_bytes, w1_scale, w2_b
         def sort_x(b, r, passes, copy):
             if b not in x_sorted:
                 x_sorted[b] = work.tile([P, 2, 2, 2, P], U32, name="x_sorted_tile", align_bytes=64, bufs=4)
-            words = x_raw[b][:, r, :].bitcast(U32).rearrange("p (c m u) -> p c u m", c=2, u=2)
-            copy(out=x_sorted[b][:, r, passes], in_=words[:, passes])
+            words = x_raw[b][:, r, :].bitcast(U32).rearrange("p (c q i u) -> p c q u i", c=2, i=4, u=2)
+            target = x_sorted[b][:, r].rearrange("p c u (q i) -> p c q u i", i=4)
+            copy(out=target[:, passes], in_=words[:, passes])
             for c in range(passes.start, passes.stop):
                 is_sorted.add((b, r, c))
 
@@ -170,8 +171,8 @@ def tile_sensor_residual_squared_d7_kernel(tc, x, g, a, w1_bytes, w1_scale, w2_b
             if r == 0:
                 pair_tile[b] = work.tile([P, 3, HALF], F32, name="pair_tile", align_bytes=64, bufs=5)
             nc.scalar.copy(
-                out=x_laced(b)[:, :, 128 * r : 128 * r + 128, :].bitcast(F32),
-                in_=bank[:].rearrange("p c u n -> p c n u"),
+                out=x_laced(b)[:, :, 128 * r : 128 * r + 128, :].bitcast(F32).rearrange("p c (n e) u -> p c n u e", e=2),
+                in_=bank[:].rearrange("p c u (n e) -> p c n u e", e=2),
             )
 
         def turn_and_lace_x(b):
@@ -208,9 +209,9 @@ def tile_sensor_residual_squared_d7_kernel(tc, x, g, a, w1_bytes, w1_scale, w2_b
             if r == 0:
                 h_tile[b] = work.tile([P, 2, P, 4], BF16, name="h_tile", align_bytes=64, bufs=2)
             nc.vector.tensor_tensor(
-                out=h_tile[b][:, r],
-                in0=h_sums[b, r][:].rearrange("p u n -> p n u"),
-                in1=a_cols[:].unsqueeze(1).to_broadcast([P, P, 4]),
+                out=h_tile[b][:, r].rearrange("p (n e) u -> p n u e", e=2),
+                in0=h_sums[b, r][:].rearrange("p u (n e) -> p n u e", e=2),
+                in1=a_cols[:].unsqueeze(1).unsqueeze(3).to_broadcast([P, P // 2, 4, 2]),
                 op=ALU.mult,
             )
 

@@ -34,7 +34,7 @@ def tile_sensor_residual_squared_d7_kernel(tc, x, g, a, w1_bytes, w1_scale, w2_b
         ctx.enter_context(tc.manual_schedule())
 
         x_raw, x_sorted, pair_tile, x_codes, x_scales = {}, {}, {}, {}, {}
-        h_sums, h_tile, h_codes, h_scales = {}, {}, {}, {}
+        h_sums, h_home, h_tile, h_codes, h_scales = {}, {}, {}, {}, {}
         xg, y_turned, y_direct, e_turned, result = {}, {}, {}, {}, {}
 
         is_sorted = set()
@@ -165,11 +165,11 @@ def tile_sensor_residual_squared_d7_kernel(tc, x, g, a, w1_bytes, w1_scale, w2_b
             return bank
 
         def x_laced(b):
-            return pair_tile[b][:, 0:2, :].bitcast(BF16).rearrange("p c (n t) -> p c n t", t=4)
+            return pair_tile[b][:].bitcast(BF16).rearrange("p c (n t) -> p c n t", t=4)
 
         def lace_x(b, r, bank):
             if r == 0:
-                pair_tile[b] = work.tile([P, 3, HALF], F32, name="pair_tile", align_bytes=64, bufs=5)
+                pair_tile[b] = work.tile([P, 2, HALF], F32, name="pair_tile", align_bytes=64, bufs=5)
             nc.scalar.copy(
                 out=x_laced(b)[:, :, 128 * r : 128 * r + 128, :].bitcast(F32).rearrange("p c (n e) u -> p c n u e", e=2),
                 in_=bank[:].rearrange("p c u (n e) -> p c n u e", e=2),
@@ -207,7 +207,8 @@ def tile_sensor_residual_squared_d7_kernel(tc, x, g, a, w1_bytes, w1_scale, w2_b
 
         def weigh(b, r):
             if r == 0:
-                h_tile[b] = work.tile([P, 2, P, 4], BF16, name="h_tile", align_bytes=64, bufs=2)
+                h_home[b] = work.tile([P, 2, HALF], F32, name="h_home_tile", align_bytes=64, bufs=5)
+                h_tile[b] = h_home[b][:, 0, :].bitcast(BF16).rearrange("p (r n t) -> p r n t", r=2, t=4)
             nc.vector.tensor_tensor(
                 out=h_tile[b][:, r].rearrange("p (n e) u -> p n u e", e=2),
                 in0=h_sums[b, r][:].rearrange("p u (n e) -> p n u e", e=2),
@@ -221,14 +222,14 @@ def tile_sensor_residual_squared_d7_kernel(tc, x, g, a, w1_bytes, w1_scale, w2_b
             nc.vector.quantize_mx(
                 out=h_codes[b][:].bitcast(X4),
                 scales=h_scales[b][:],
-                in_=h_tile[b][:].rearrange("p r n t -> p (r n t)"),
+                in_=h_tile[b].rearrange("p r n t -> p (r n t)"),
             )
 
         def standardise(b):
             if b == 1:
                 xg[b] = laced[1, DIRECT][:].rearrange("p (r n) t -> p r (n t)", r=2).bitcast(F32)
             else:
-                xg[b] = pair_tile[b][:, 1:3, :]
+                xg[b] = h_home[b - 1][:]
             nc.gpsimd.tensor_tensor(
                 out=xg[b],
                 in0=x_raw[b][:, :, HALF:],

@@ -33,11 +33,13 @@ def tile_sensor_residual_squared_d7_kernel(tc, x, g, a, w1_bytes, w1_scale, w2_b
         psum = ctx.enter_context(tc.psum_pool(name="psum", bufs=1))
         ctx.enter_context(tc.manual_schedule())
 
-        x_raw, x_sorted, pair_tile, x_codes, x_scales = {}, {}, {}, {}, {}
-        h_sums, h_home, h_tile, h_codes, h_scales = {}, {}, {}, {}, {}
-        xg, y_turned, y_direct, e_turned, result = {}, {}, {}, {}, {}
-
+        x_raw, x_sorted, x_quad, x_codes, x_scales = {}, {}, {}, {}, {}
+        h_sums, h_home, h_codes, h_scales = {}, {}, {}, {}
+        xg, y_turned, y_direct, e_turned, result, back_banks = {}, {}, {}, {}, {}, {}
         is_sorted = set()
+
+        def inside(b):
+            return 0 <= b < PAIRS
 
         def mx_bank(shape):
             return psum.tile(shape, F32, name="mx_bank", bufs=MX_BANKS)
@@ -45,13 +47,16 @@ def tile_sensor_residual_squared_d7_kernel(tc, x, g, a, w1_bytes, w1_scale, w2_b
         def turn_bank(shape):
             return psum.tile(shape, F32, name="turn_bank", bufs=TURN_BANKS)
 
+        def row_tile(shape, dtype):
+            return work.tile(shape, dtype, name="row_tile", align_bytes=64, bufs=8)
+
         def load_x(b):
             tile = keep.tile([P, 2, D], BF16, name="x_tile", align_bytes=64, bufs=PAIRS)
             nc.sync.dma_start(out=tile[:].rearrange("p r d -> p (r d)"), in_=x_pairs[b])
             x_raw[b] = tile
 
         w_raw = {(w, c): keep.tile([P, 4, R], U8, name="w_raw", align_bytes=64, bufs=4) for w in range(2) for c in range(2)}
-        scale_cols = [keep.tile([P, 2, 4], F32, name="scale_cols", bufs=2) for w in range(2)]
+        scale_cols = {(w, c): keep.tile([P, 4], F32, name="scale_cols", bufs=4) for w in range(2) for c in range(2)}
         a_cols = keep.tile([P, 4], BF16, name="a_cols")
         g_cols = keep.tile([P, 4], BF16, name="g_cols")
         g_rows = keep.tile([P, HALF], BF16, name="g_rows", align_bytes=64)
@@ -60,33 +65,44 @@ def tile_sensor_residual_squared_d7_kernel(tc, x, g, a, w1_bytes, w1_scale, w2_b
             rows = (w1_bytes, w2_bytes)[w].rearrange("(c p t) n -> c p (t n)", p=P, t=4)
             nc.sync.dma_start(out=w_raw[w, c][:].rearrange("p t n -> p (t n)"), in_=rows[c])
 
-        def load_scales(queue, w):
-            block_rows = (w1_scale, w2_scale)[w].rearrange("(c q) j -> q c j", q=4)
-            for q in range(4):
-                queue.dma_start(out=scale_cols[w][32 * q : 32 * q + 32], in_=block_rows[q].partition_broadcast(32))
+        def load_scales(queue, w, c):
+            block_rows = (w1_scale, w2_scale)[w][4 * c : 4 * c + 4]
+            queue.dma_start(out=scale_cols[w, c][:], in_=block_rows.unsqueeze(1).broadcast_to([4, 32, 4]))
 
-        load_scales(nc.scalar, 0)
+        def load_a(queue):
+            queue.dma_start(out=a_cols[:], in_=a.rearrange("(p t) -> p t", t=4))
+
+        def load_g_rows(queue):
+            queue.dma_start(out=g_rows[:], in_=g[HALF:].partition_broadcast(P))
+
+        def load_g_cols(queue):
+            queue.dma_start(out=g_cols[:], in_=g[0:HALF].rearrange("(p t) -> p t", t=4))
+
+        for w in range(2):
+            for c in range(2):
+                load_scales(nc.scalar, w, c)
         for c in range(2):
             load_w(0, c)
         for b in range(2):
             load_x(b)
-        load_scales(nc.sync, 1)
         for c in range(2):
             load_w(1, c)
-        nc.sync.dma_start(out=a_cols[:], in_=a.rearrange("(p t) -> p t", t=4))
-        nc.sync.dma_start(out=g_rows[:], in_=g[HALF:].partition_broadcast(P))
+        load_a(nc.sync)
+        load_g_rows(nc.sync)
         for b in range(2, 4):
             load_x(b)
-        nc.sync.dma_start(out=g_cols[:], in_=g[0:HALF].rearrange("(p t) -> p t", t=4))
+        load_g_cols(nc.sync)
         for b in range(4, PAIRS):
             load_x(b)
 
         ident = keep.tile([P, P], F32, name="ident", align_bytes=64)
         make_identity(nc, ident[:])
 
-        w1_wide = [keep.tile([P, 4, R], BF16, name="w1_wide", align_bytes=64, bufs=2) for c in range(2)]
-        w2_scaled = [keep.tile([P, 4, R], BF16, name="w2_scaled", align_bytes=64, bufs=2) for c in range(2)]
-        laced = {(w, c): keep.tile([P, R, 4], BF16, name="laced", align_bytes=64, bufs=4) for w in range(2) for c in range(2)}
+        w1_wide = [row_tile([P, 4, R], BF16) for c in range(2)]
+        laced = {(0, c): row_tile([P, R, 4], BF16) for c in range(2)}
+        w2_scaled = [row_tile([P, 4, R], BF16) for c in range(2)]
+        for c in range(2):
+            laced[1, c] = row_tile([P, R, 4], BF16)
         w_codes = [keep.tile([P, 2, R], U32, name="w_codes", align_bytes=64, bufs=2) for w in range(2)]
         w_scales = [keep.tile([P, 2, R], U8, name="w_scales", align_bytes=64, bufs=2) for w in range(2)]
         w2_banks = {}
@@ -101,31 +117,30 @@ def tile_sensor_residual_squared_d7_kernel(tc, x, g, a, w1_bytes, w1_scale, w2_b
         def lace_w1(c, j, on_scalar):
             out_ = laced[0, c][:].rearrange("p (u m) t -> p m u t", u=4)[:, 32 * j : 32 * j + 32]
             in_ = w1_wide[c][:, :, 128 * j : 128 * j + 128].rearrange("p t (m u) -> p m u t", u=4)
-            scale = scale_cols[0][:, c, j : j + 1]
+            scale = scale_cols[0, c][:, j : j + 1]
             if on_scalar:
                 nc.scalar.activation(out=out_, in_=in_, func=ACT.Copy, scale=scale)
             else:
                 nc.vector.tensor_scalar(out=out_, in0=in_, scalar1=scale, scalar2=None, op0=ALU.mult)
 
-        def scale_w2(c):
-            for t in range(4):
+        def scale_w2(c, rows, on_scalar):
+            for t in rows:
                 for j in range(4):
                     columns = slice(128 * j, 128 * j + 128)
                     out_, in_ = w2_scaled[c][:, t, columns], w_raw[1, c][:, t, columns].bitcast(E4M3)
-                    scale = scale_cols[1][:, c, j : j + 1]
-                    if c == TURNED:
-                        nc.vector.tensor_scalar(out=out_, in0=in_, scalar1=scale, scalar2=None, op0=ALU.mult)
-                    else:
+                    scale = scale_cols[1, c][:, j : j + 1]
+                    if on_scalar:
                         nc.scalar.activation(out=out_, in_=in_, func=ACT.Copy, scale=scale)
+                    else:
+                        nc.vector.tensor_scalar(out=out_, in0=in_, scalar1=scale, scalar2=None, op0=ALU.mult)
 
-        def turn_w2(c):
-            for i in range(2):
-                bank = turn_bank([P, 2, 2, P])
-                for k in range(2):
-                    words = w2_scaled[c][:, 2 * i + k, :].bitcast(F32)
-                    for u in range(2):
-                        nc.tensor.transpose(bank[:, k, u, :], words[:, u::2], ident[:])
-                w2_banks[c, i] = bank
+        def turn_w2(c, i, new_bank):
+            bank = new_bank([P, 2, 2, P])
+            for k in range(2):
+                words = w2_scaled[c][:, 2 * i + k, :].bitcast(F32)
+                for u in range(2):
+                    nc.tensor.transpose(bank[:, k, u, :], words[:, u::2], ident[:])
+            w2_banks[c, i] = bank
 
         def lace_w2(c, i, copy):
             words, bank = laced[1, c][:].bitcast(F32), w2_banks[c, i]
@@ -143,41 +158,42 @@ def tile_sensor_residual_squared_d7_kernel(tc, x, g, a, w1_bytes, w1_scale, w2_b
                 in_=laced[w, c][:].rearrange("p n t -> p (n t)"),
             )
 
-        def sort_x(b, r, passes, copy):
+        def sort_x(b, parts, copy):
             if b not in x_sorted:
-                x_sorted[b] = work.tile([P, 2, 2, 2, P], U32, name="x_sorted_tile", align_bytes=64, bufs=4)
-            words = x_raw[b][:, r, :].bitcast(U32).rearrange("p (c q i u) -> p c q u i", c=2, i=4, u=2)
-            target = x_sorted[b][:, r].rearrange("p c u (q i) -> p c q u i", i=4)
-            copy(out=target[:, passes], in_=words[:, passes])
-            for c in range(passes.start, passes.stop):
-                is_sorted.add((b, r, c))
+                x_sorted[b] = work.tile([P, 4, 2, P], U32, name="x_sorted_tile", align_bytes=64, bufs=4)
+            words = x_raw[b][:].rearrange("p r d -> p (r d)").bitcast(U32)
+            words = words.rearrange("p (c q i u) -> p c q u i", c=4, i=4, u=2)
+            target = x_sorted[b][:].rearrange("p c u (q i) -> p c q u i", i=4)
+            copy(out=target[:, parts], in_=words[:, parts])
+            for part in range(parts.start, parts.stop):
+                is_sorted.add((b, part))
 
-        def turn_x(b, r):
-            bank = turn_bank([P, 2, 2, P])
+        def turn_x(b, r, new_bank):
+            bank = new_bank([P, 2, 2, P])
             words = x_raw[b][:, r, :].bitcast(F32)
             for c in range(2):
                 for u in range(2):
-                    if (b, r, c) in is_sorted:
-                        source = x_sorted[b][:, r, c, u, :].bitcast(F32)
+                    if (b, 2 * r + c) in is_sorted:
+                        source = x_sorted[b][:, 2 * r + c, u, :].bitcast(F32)
                     else:
                         source = words[:, 256 * c + u : 256 * (c + 1) : 2]
                     nc.tensor.transpose(bank[:, c, u, :], source, ident[:])
             return bank
 
         def x_laced(b):
-            return pair_tile[b][:].bitcast(BF16).rearrange("p c (n t) -> p c n t", t=4)
+            return x_quad[b // 2][:, b % 2]
 
-        def lace_x(b, r, bank):
-            if r == 0:
-                pair_tile[b] = work.tile([P, 2, HALF], F32, name="pair_tile", align_bytes=64, bufs=5)
-            nc.scalar.copy(
+        def lace_x(b, r, bank, copy):
+            if b // 2 not in x_quad:
+                x_quad[b // 2] = work.tile([P, 2, 2, 256, 4], BF16, name="x_quad_tile", align_bytes=64, bufs=3)
+            copy(
                 out=x_laced(b)[:, :, 128 * r : 128 * r + 128, :].bitcast(F32).rearrange("p c (n e) u -> p c n u e", e=2),
                 in_=bank[:].rearrange("p c u (n e) -> p c n u e", e=2),
             )
 
         def turn_and_lace_x(b):
             for r in range(2):
-                lace_x(b, r, turn_x(b, r))
+                lace_x(b, r, turn_x(b, r, turn_bank), nc.scalar.copy)
 
         def quantize_x(b):
             x_codes[b] = work.tile([P, 2, 256], U32, name="x_codes_tile", align_bytes=64)
@@ -205,123 +221,134 @@ def tile_sensor_residual_squared_d7_kernel(tc, x, g, a, w1_bytes, w1_scale, w2_b
                     )
             h_sums[b, r] = bank
 
+        def h_values(b):
+            return h_home[b][:, 0, :].bitcast(BF16)
+
         def weigh(b, r):
             if r == 0:
                 h_home[b] = work.tile([P, 2, HALF], F32, name="h_home_tile", align_bytes=64, bufs=5)
-                h_tile[b] = h_home[b][:, 0, :].bitcast(BF16).rearrange("p (r n t) -> p r n t", r=2, t=4)
             nc.vector.tensor_tensor(
-                out=h_tile[b][:, r].rearrange("p (n e) u -> p n u e", e=2),
+                out=h_values(b)[:, HALF * r : HALF * (r + 1)].rearrange("p (n e u) -> p n u e", e=2, u=4),
                 in0=h_sums[b, r][:].rearrange("p u (n e) -> p n u e", e=2),
                 in1=a_cols[:].unsqueeze(1).unsqueeze(3).to_broadcast([P, P // 2, 4, 2]),
                 op=ALU.mult,
             )
 
-        def quantize_h(b):
-            h_codes[b] = work.tile([P, 256], U32, name="h_codes_tile", align_bytes=64)
-            h_scales[b] = work.tile([P, 256], U8, name="h_scales_tile", align_bytes=64)
+        def quantize_h(b, tiles=(0, 1)):
+            if b // 2 not in h_codes:
+                h_codes[b // 2] = work.tile([P, HALF], U32, name="h_codes_tile", align_bytes=64)
+                h_scales[b // 2] = work.tile([P, HALF], U8, name="h_scales_tile", align_bytes=64)
+            tokens = tokens_of(b, tiles)
             nc.vector.quantize_mx(
-                out=h_codes[b][:].bitcast(X4),
-                scales=h_scales[b][:],
-                in_=h_tile[b].rearrange("p r n t -> p (r n t)"),
+                out=h_codes[b // 2][:, tokens].bitcast(X4),
+                scales=h_scales[b // 2][:, tokens],
+                in_=h_values(b)[:, HALF * tiles[0] : HALF * (tiles[-1] + 1)],
             )
 
-        def standardise(b):
-            if b == 1:
-                xg[b] = laced[1, DIRECT][:].rearrange("p (r n) t -> p r (n t)", r=2).bitcast(F32)
-            else:
-                xg[b] = h_home[b - 1][:]
-            nc.gpsimd.tensor_tensor(
-                out=xg[b],
-                in0=x_raw[b][:, :, HALF:],
-                in1=g_rows[:].unsqueeze(1).to_broadcast([P, 2, HALF]),
+        def standardise(b, home, tiles=slice(0, 2), engine=nc.gpsimd):
+            for r in range(tiles.start, tiles.stop):
+                xg[b, r] = home[:, r - tiles.start, :]
+            engine.tensor_tensor(
+                out=home,
+                in0=x_raw[b][:, tiles, HALF:],
+                in1=g_rows[:].unsqueeze(1).to_broadcast([P, tiles.stop - tiles.start, HALF]),
                 op=ALU.mult,
             )
 
-        first_xg = {}
+        def result_of(b, r):
+            if (b, r) not in result:
+                result[b, r] = row_tile([P, D], F32)
+            return result[b, r]
 
-        def standardise_first(r, engine, home):
-            first_xg[r] = home
-            engine.tensor_tensor(out=home, in0=x_raw[0][:, r, HALF:], in1=g_rows[:], op=ALU.mult)
+        on_tensor = set()
+        g_wide = keep.tile([P, 4], F32, name="g_wide")
+        g_diag = keep.tile([P, 4, P], BF16, name="g_diag", align_bytes=64)
 
-        def result_of(b):
-            if b not in result:
-                result[b] = work.tile([P, 2, D], F32, name="result_tile", align_bytes=64)
-            return result[b]
+        def make_g_diag(planes):
+            nc.scalar.activation(out=g_wide[:], in_=g_cols[:], func=ACT.Copy)
+            for t in planes:
+                nc.scalar.activation(out=g_diag[:, t, :], in_=ident[:], func=ACT.Copy, scale=g_wide[:, t : t + 1])
 
-        def on_tensor(b):
-            return not inside(b + 3)
+        def tokens_of(b, tiles):
+            return slice(256 * (b % 2) + 128 * tiles[0], 256 * (b % 2) + 128 * (tiles[-1] + 1))
 
-        g_first = keep.tile([P, 1], F32, name="g_first")
-        g_diag = keep.tile([P, P], BF16, name="g_diag", align_bytes=64)
-
-        def make_g_diag():
-            nc.scalar.activation(out=g_first[:], in_=g_cols[:, 0:1], func=ACT.Copy)
-            nc.scalar.activation(out=g_diag[:], in_=ident[:], func=ACT.Copy, scale=g_first[:])
-
-        def product_turned(b, i):
-            bank = mx_bank([P, 2, 256])
-            for k in range(2):
-                columns = slice(128 * (2 * i + k), 128 * (2 * i + k) + 128)
+        def product_turned(b, tiles, planes):
+            bank = mx_bank([P, len(planes), 128 * len(tiles)])
+            tokens = tokens_of(b, tiles)
+            for k, t in enumerate(planes):
+                columns = slice(128 * t, 128 * t + 128)
                 nc.tensor.matmul_mx(
                     out=bank[:, k, :],
                     lhsT=w_codes[1][:, TURNED, columns].bitcast(X4),
                     lhsT_scale=w_scales[1][:, TURNED, columns],
-                    rhs=h_codes[b][:].bitcast(X4),
-                    rhs_scale=h_scales[b][:],
+                    rhs=h_codes[b // 2][:, tokens].bitcast(X4),
+                    rhs_scale=h_scales[b // 2][:, tokens],
                     start=True,
                     stop=True,
                 )
-            y_turned[b, i] = bank
+                y_turned[b, tiles, t] = (bank, k)
 
-        def subtract_turned(b, i):
-            if i == 0:
-                e_turned[b] = work.tile([P, 4, 256], F32, name="e_turned_tile", align_bytes=64, bufs=2)
-            for k in range(2):
-                t = 2 * i + k
-                if t == 0 and on_tensor(b):
-                    continue
-                nc.vector.scalar_tensor_tensor(
-                    out=e_turned[b][:, t, :],
-                    in0=x_laced(b)[:, TURNED, :, t],
-                    scalar=g_cols[:, t : t + 1],
-                    in1=y_turned[b, i][:, k, :],
-                    op0=ALU.mult,
-                    op1=ALU.subtract,
-                )
+        def e_planes(b, tiles):
+            if b // 2 not in e_turned:
+                e_turned[b // 2] = work.tile([P, 4, HALF], F32, name="e_turned_tile", align_bytes=64, bufs=2)
+            return e_turned[b // 2][:, :, tokens_of(b, tiles)]
 
-        def negate_first(b):
-            nc.scalar.activation(out=e_turned[b][:, 0, :], in_=y_turned[b, 0][:, 0, :], func=ACT.Copy, scale=-1.0)
+        def subtract_turned(b, tiles, t):
+            bank, k = y_turned[b, tiles, t]
+            nc.vector.scalar_tensor_tensor(
+                out=e_planes(b, tiles)[:, t, :],
+                in0=x_laced(b)[:, TURNED, 128 * tiles[0] : 128 * (tiles[-1] + 1), t],
+                scalar=g_cols[:, t : t + 1],
+                in1=bank[:, k, :],
+                op0=ALU.mult,
+                op1=ALU.subtract,
+            )
 
-        back_banks = {}
+        def negate(b, tiles, planes):
+            bank, k = y_turned[b, tiles, planes[0]]
+            for r in tiles:
+                for t in planes:
+                    on_tensor.add((b, r, t))
+            nc.scalar.activation(
+                out=e_planes(b, tiles)[:, planes[0] : planes[-1] + 1, :],
+                in_=bank[:, k : k + len(planes), :],
+                func=ACT.Copy,
+                scale=-1.0,
+            )
 
-        def open_back(b):
-            for r in range(2):
-                back_banks[b, r] = turn_bank([P, 4, P])
-                if on_tensor(b):
-                    x_first = x_laced(b)[:, TURNED, 128 * r : 128 * r + 128, 0]
-                    nc.tensor.matmul(back_banks[b, r][:, 0, :], x_first, g_diag[:], start=True, stop=False)
+        def open_back(b, r, new_bank=turn_bank):
+            back_banks[b, r] = new_bank([P, 4, P])
+            planes = [t for t in range(4) if (b, r, t) in on_tensor]
+            for t in planes:
+                x_plane = x_laced(b)[:, TURNED, 128 * r : 128 * r + 128, t]
+                nc.tensor.matmul(back_banks[b, r][:, t, :], x_plane, g_diag[:, t, :], start=(t == planes[0]), stop=False)
 
         def turn_back(b, r):
             bank = back_banks[b, r]
-            for t in range(4):
-                source = e_turned[b][:, t, 128 * r : 128 * r + 128]
-                if t == 0 and on_tensor(b):
-                    nc.tensor.matmul(bank[:, t, :], source, ident[:], start=False, stop=True, is_transpose=True)
+            planes = [t for t in range(4) if (b, r, t) in on_tensor]
+            first = 256 * (b % 2) + 128 * r
+            for t in planes + [t for t in range(4) if t not in planes]:
+                source = e_turned[b // 2][:, t, first : first + 128]
+                if t in planes:
+                    nc.tensor.matmul(bank[:, t, :], source, ident[:], start=False, stop=(t == planes[-1]), is_transpose=True)
                 else:
                     nc.tensor.transpose(bank[:, t, :], source, ident[:])
+
+        def square_turned(b, r):
             nc.scalar.activation(
-                out=result_of(b)[:, r, 0:HALF].rearrange("p (m t) -> p m t", t=4),
-                in_=bank[:].rearrange("p t m -> p m t"),
+                out=result_of(b, r)[:, 0:HALF].rearrange("p (m e t) -> p m t e", e=2, t=4),
+                in_=back_banks[b, r][:].rearrange("p t (m e) -> p m t e", e=2),
                 func=ACT.Square,
             )
 
         def product_direct(b, r):
-            tokens = slice(128 * r, 128 * r + 128)
+            first = 256 * (b % 2) + 128 * r
+            tokens = slice(first, first + 128)
             bank = mx_bank([P, HALF])
             nc.tensor.matmul_mx(
                 out=bank[:],
-                lhsT=h_codes[b][:, tokens].bitcast(X4),
-                lhsT_scale=h_scales[b][:, tokens],
+                lhsT=h_codes[b // 2][:, tokens].bitcast(X4),
+                lhsT_scale=h_scales[b // 2][:, tokens],
                 rhs=w_codes[1][:, DIRECT, :].bitcast(X4),
                 rhs_scale=w_scales[1][:, DIRECT, :],
                 start=True,
@@ -329,115 +356,123 @@ def tile_sensor_residual_squared_d7_kernel(tc, x, g, a, w1_bytes, w1_scale, w2_b
             )
             y_direct[b, r] = bank
 
-        def subtract_direct(b, r):
-            nc.vector.tensor_tensor(
-                out=result_of(b)[:, r, HALF:], in0=xg[b][:, r, :] if b else first_xg[r], in1=y_direct[b, r][:], op=ALU.subtract
-            )
+        def subtract_direct(b, r, columns=slice(0, HALF)):
+            tile = xg[b, r][:, columns]
+            nc.vector.tensor_tensor(out=tile, in0=tile, in1=y_direct[b, r][:, columns], op=ALU.subtract)
 
-        def square_direct(b, r):
-            tile = result[b][:, r, HALF:]
-            if b < PAIRS - 1:
-                nc.scalar.activation(out=tile, in_=tile, func=ACT.Square)
+        def square_direct(b, r, engine=nc.scalar, columns=slice(0, HALF)):
+            tile, target = xg[b, r][:, columns], result_of(b, r)[:, HALF:][:, columns]
+            if engine is nc.scalar:
+                nc.scalar.activation(out=target, in_=tile, func=ACT.Square)
             else:
-                nc.vector.tensor_tensor(out=tile, in0=tile, in1=tile, op=ALU.mult)
+                engine.tensor_tensor(out=target, in0=tile, in1=tile, op=ALU.mult)
 
         def store(b, r, sensors):
-            nc.sync.dma_start(out=out_pairs[b][:, r, sensors], in_=result[b][:, r, sensors])
+            nc.sync.dma_start(out=out_pairs[b][:, r, sensors], in_=result[b, r][:, sensors])
 
-        def inside(b):
-            return 0 <= b < PAIRS
+        both = (0, 1)
+        whole, turned, direct, last = slice(0, D), slice(0, HALF), slice(HALF, D), PAIRS - 1
 
         widen_w1()
         for j in (2, 3):
             lace_w1(1, j, on_scalar=True)
-        banks = [(b, r, turn_x(b, r)) for b in range(2) for r in range(2)]
+        banks = [(b, r, turn_x(b, r, turn_bank)) for b in range(2) for r in range(2)]
         for j in range(4):
             lace_w1(0, j, on_scalar=False)
         for j in (0, 1):
             lace_w1(1, j, on_scalar=False)
         for args in banks:
-            lace_x(*args)
+            lace_x(*args, nc.scalar.copy)
         for c in range(2):
             quantize_w(0, c)
         quantize_x(0)
-        for c in range(2):
-            scale_w2(c)
+        scale_w2(TURNED, range(4), on_scalar=False)
+        scale_w2(DIRECT, range(4), on_scalar=True)
         first_product(0, 0)
-        turn_w2(TURNED)
+        for i in range(2):
+            turn_w2(TURNED, i, turn_bank)
         first_product(0, 1)
         quantize_x(1)
-        standardise_first(1, nc.gpsimd, pair_tile[1][:, 1, :])
+        standardise(0, x_quad[0][:, 1:2, DIRECT].rearrange("p b n t -> p b (n t)").bitcast(F32), slice(1, 2))
         weigh(0, 0)
         lace_w2(TURNED, 0, nc.vector.tensor_copy)
         lace_w2(TURNED, 1, nc.scalar.copy)
         weigh(0, 1)
-        turn_w2(DIRECT)
+        for i in range(2):
+            turn_w2(DIRECT, i, turn_bank)
         quantize_w(1, TURNED)
         quantize_h(0)
-        standardise_first(0, nc.vector, pair_tile[0][:, 1, :])
+        standardise(0, x_quad[0][:, 0:1, DIRECT].rearrange("p b n t -> p b (n t)").bitcast(F32), slice(0, 1), nc.vector)
         for i in range(2):
             lace_w2(DIRECT, i, nc.scalar.copy)
         turn_and_lace_x(2)
         quantize_w(1, DIRECT)
-        standardise(1)
-        sort_x(3, 0, slice(0, 2), nc.scalar.copy)
-        make_g_diag()
+        standardise(1, laced[1, DIRECT][:].rearrange("p (r n) t -> p r (n t)", r=2).bitcast(F32))
+        sort_x(3, slice(0, 2), nc.scalar.copy)
+        make_g_diag((2, 3))
 
-        whole, turned, direct, last = slice(0, D), slice(0, HALF), slice(HALF, D), PAIRS - 1
-        for s in range(PAIRS):
+        for s in range(PAIRS - 1):
             if s > 0:
                 product_direct(s - 1, 1)
-            for i in range(2):
-                product_turned(s, i)
-            if s < last:
-                first_product(s + 1, 0)
-            else:
-                product_direct(s, 0)
+            product_turned(s, both, (0, 1))
+            product_turned(s, both, (2, 3))
+            first_product(s + 1, 0)
             if s > 0:
                 subtract_direct(s - 1, 1)
-            if s < last:
-                first_product(s + 1, 1)
-            else:
-                product_direct(s, 1)
-            subtract_turned(s, 0)
-            if on_tensor(s):
-                negate_first(s)
+            first_product(s + 1, 1)
+            for t in (0, 1):
+                subtract_turned(s, both, t)
+            if not inside(s + 3):
+                negate(s, both, (2, 3))
             if s > 0:
                 square_direct(s - 1, 1)
-                store(s - 1, 1, whole if s < last else direct)
-            if s < last:
-                product_direct(s, 0)
-            subtract_turned(s, 1)
-            if s < last:
-                for r in range(2):
-                    weigh(s + 1, r)
+                store(s - 1, 1, whole if s < last - 1 else direct)
+            product_direct(s, 0)
+            if inside(s + 3):
+                for t in (2, 3):
+                    subtract_turned(s, both, t)
+            for r in range(2):
+                weigh(s + 1, r)
             if s > 0 and inside(s + 3):
-                sort_x(s + 3, 1, slice(0, 2), nc.scalar.copy)
+                sort_x(s + 3, slice(2, 4), nc.scalar.copy)
             subtract_direct(s, 0)
-            if s < last:
-                quantize_h(s + 1)
-                if inside(s + 2):
-                    quantize_x(s + 2)
-                    standardise(s + 2)
-                if inside(s + 5):
-                    sort_x(s + 5, 0, slice(0, 1), nc.gpsimd.tensor_copy)
-                open_back(s)
-                for r in range(2):
-                    turn_back(s, r)
-                    if s == last - 1:
-                        store(s, r, turned)
-                square_direct(s, 0)
-                store(s, 0, whole if s < last - 1 else direct)
+            quantize_h(s + 1)
+            if inside(s + 2):
+                quantize_x(s + 2)
+                standardise(s + 2, h_home[s + 1][:])
+            if inside(s + 5):
+                sort_x(s + 5, slice(0, 1), nc.gpsimd.tensor_copy)
+            for r in range(2):
+                open_back(s, r)
+            for r in range(2):
+                turn_back(s, r)
+                square_turned(s, r)
+                if s >= last - 2:
+                    store(s, r, turned)
+            square_direct(s, 0, nc.scalar if s < last - 1 else nc.gpsimd)
+            store(s, 0, whole if s < last - 2 else direct)
             if inside(s + 3):
                 turn_and_lace_x(s + 3)
 
-        open_back(last)
-        square_direct(last, 0)
-        store(last, 0, direct)
-        subtract_direct(last, 1)
-        turn_back(last, 0)
-        store(last, 0, turned)
-        turn_back(last, 1)
-        store(last, 1, turned)
-        square_direct(last, 1)
-        store(last, 1, direct)
+        product_direct(14, 1)
+        product_turned(15, both, (2, 3))
+        product_turned(15, both, (0, 1))
+        product_direct(15, 0)
+        subtract_direct(14, 1)
+        product_direct(15, 1)
+        negate(15, both, (2, 3))
+        for t in (0, 1):
+            subtract_turned(15, both, t)
+        square_direct(14, 1)
+        store(14, 1, direct)
+        for r in range(2):
+            open_back(15, r)
+        for r in range(2):
+            subtract_direct(15, r)
+        for r in range(2):
+            turn_back(15, r)
+        for r in range(2):
+            square_direct(15, r, nc.vector)
+            square_turned(15, r)
+            store(15, r, turned)
+            store(15, r, direct)

@@ -56,7 +56,7 @@ def tile_sensor_residual_squared_d7_kernel(tc, x, g, a, w1_bytes, w1_scale, w2_b
             x_raw[b] = tile
 
         w_raw = {(w, c): keep.tile([P, 4, R], U8, name="w_raw", align_bytes=64, bufs=4) for w in range(2) for c in range(2)}
-        scale_cols = {(w, c): keep.tile([P, 4], F32, name="scale_cols", bufs=4) for w in range(2) for c in range(2)}
+        scale_cols = [keep.tile([P, 2, 4], F32, name="scale_cols", bufs=2) for w in range(2)]
         a_cols = keep.tile([P, 4], BF16, name="a_cols")
         g_cols = keep.tile([P, 4], BF16, name="g_cols")
         g_rows = keep.tile([P, HALF], BF16, name="g_rows", align_bytes=64)
@@ -65,9 +65,10 @@ def tile_sensor_residual_squared_d7_kernel(tc, x, g, a, w1_bytes, w1_scale, w2_b
             rows = (w1_bytes, w2_bytes)[w].rearrange("(c p t) n -> c p (t n)", p=P, t=4)
             nc.sync.dma_start(out=w_raw[w, c][:].rearrange("p t n -> p (t n)"), in_=rows[c])
 
-        def load_scales(queue, w, c):
-            block_rows = (w1_scale, w2_scale)[w][4 * c : 4 * c + 4]
-            queue.dma_start(out=scale_cols[w, c][:], in_=block_rows.unsqueeze(1).broadcast_to([4, 32, 4]))
+        def load_scales(queue, w):
+            block_rows = (w1_scale, w2_scale)[w].rearrange("(c q) j -> q c j", q=4)
+            for q in range(4):
+                queue.dma_start(out=scale_cols[w][32 * q : 32 * q + 32], in_=block_rows[q].partition_broadcast(32))
 
         def load_a(queue):
             queue.dma_start(out=a_cols[:], in_=a.rearrange("(p t) -> p t", t=4))
@@ -78,13 +79,12 @@ def tile_sensor_residual_squared_d7_kernel(tc, x, g, a, w1_bytes, w1_scale, w2_b
         def load_g_cols(queue):
             queue.dma_start(out=g_cols[:], in_=g[0:HALF].rearrange("(p t) -> p t", t=4))
 
-        for w in range(2):
-            for c in range(2):
-                load_scales(nc.scalar, w, c)
+        load_scales(nc.scalar, 0)
         for c in range(2):
             load_w(0, c)
         for b in range(2):
             load_x(b)
+        load_scales(nc.sync, 1)
         for c in range(2):
             load_w(1, c)
         load_a(nc.sync)
@@ -117,7 +117,7 @@ def tile_sensor_residual_squared_d7_kernel(tc, x, g, a, w1_bytes, w1_scale, w2_b
         def lace_w1(c, j, on_scalar):
             out_ = laced[0, c][:].rearrange("p (u m) t -> p m u t", u=4)[:, 32 * j : 32 * j + 32]
             in_ = w1_wide[c][:, :, 128 * j : 128 * j + 128].rearrange("p t (m u) -> p m u t", u=4)
-            scale = scale_cols[0, c][:, j : j + 1]
+            scale = scale_cols[0][:, c, j : j + 1]
             if on_scalar:
                 nc.scalar.activation(out=out_, in_=in_, func=ACT.Copy, scale=scale)
             else:
@@ -128,7 +128,7 @@ def tile_sensor_residual_squared_d7_kernel(tc, x, g, a, w1_bytes, w1_scale, w2_b
                 for j in range(4):
                     columns = slice(128 * j, 128 * j + 128)
                     out_, in_ = w2_scaled[c][:, t, columns], w_raw[1, c][:, t, columns].bitcast(E4M3)
-                    scale = scale_cols[1, c][:, j : j + 1]
+                    scale = scale_cols[1][:, c, j : j + 1]
                     if on_scalar:
                         nc.scalar.activation(out=out_, in_=in_, func=ACT.Copy, scale=scale)
                     else:
@@ -336,8 +336,8 @@ def tile_sensor_residual_squared_d7_kernel(tc, x, g, a, w1_bytes, w1_scale, w2_b
 
         def square_turned(b, r):
             nc.scalar.activation(
-                out=result_of(b, r)[:, 0:HALF].rearrange("p (m e t) -> p m t e", e=2, t=4),
-                in_=back_banks[b, r][:].rearrange("p t (m e) -> p m t e", e=2),
+                out=result_of(b, r)[:, 0:HALF].rearrange("p (m t) -> p m t", t=4),
+                in_=back_banks[b, r][:].rearrange("p t m -> p m t"),
                 func=ACT.Square,
             )
 

@@ -272,8 +272,8 @@ def tile_sensor_residual_squared_d7_kernel(tc, x, g, a, w1_bytes, w1_scale, w2_b
         def tokens_of(b, tiles):
             return slice(256 * (b % 2) + 128 * tiles[0], 256 * (b % 2) + 128 * (tiles[-1] + 1))
 
-        def product_turned(b, tiles, planes):
-            bank = mx_bank([P, len(planes), 128 * len(tiles)])
+        def product_turned(b, tiles, planes, new_bank=mx_bank):
+            bank = new_bank([P, len(planes), 128 * len(tiles)])
             tokens = tokens_of(b, tiles)
             for k, t in enumerate(planes):
                 columns = slice(128 * t, 128 * t + 128)
@@ -412,29 +412,38 @@ def tile_sensor_residual_squared_d7_kernel(tc, x, g, a, w1_bytes, w1_scale, w2_b
         make_g_diag((2, 3))
 
         for s in range(PAIRS - 1):
+            late = not inside(s + 3)
+            lent = (2, 3) if late else (3,) if s > 0 else ()
+            kept = [t for t in (2, 3) if t not in lent]
             if s > 0:
                 product_direct(s - 1, 1)
             product_turned(s, both, (0, 1))
-            product_turned(s, both, (2, 3))
+            if len(lent) == 1:
+                product_turned(s, both, (2,))
+                product_turned(s, both, (3,), turn_bank)
+            else:
+                product_turned(s, both, (2, 3))
             first_product(s + 1, 0)
             if s > 0:
                 subtract_direct(s - 1, 1)
             first_product(s + 1, 1)
             for t in (0, 1):
                 subtract_turned(s, both, t)
-            if not inside(s + 3):
-                negate(s, both, (2, 3))
+            if lent:
+                negate(s, both, lent)
+            if s > 0 and inside(s + 3):
+                sort_x(s + 3, slice(2, 4), nc.scalar.copy)
             if s > 0:
+                if inside(s + 2):
+                    square_direct(s - 1, 0)
+                    store(s - 1, 0, whole)
                 square_direct(s - 1, 1)
                 store(s - 1, 1, whole if s < last - 1 else direct)
             product_direct(s, 0)
-            if inside(s + 3):
-                for t in (2, 3):
-                    subtract_turned(s, both, t)
+            for t in kept:
+                subtract_turned(s, both, t)
             for r in range(2):
                 weigh(s + 1, r)
-            if s > 0 and inside(s + 3):
-                sort_x(s + 3, slice(2, 4), nc.scalar.copy)
             subtract_direct(s, 0)
             quantize_h(s + 1)
             if inside(s + 2):
@@ -449,8 +458,9 @@ def tile_sensor_residual_squared_d7_kernel(tc, x, g, a, w1_bytes, w1_scale, w2_b
                 square_turned(s, r)
                 if s >= last - 2:
                     store(s, r, turned)
-            square_direct(s, 0, nc.scalar if s < last - 1 else nc.gpsimd)
-            store(s, 0, whole if s < last - 2 else direct)
+            if not inside(s + 3):
+                square_direct(s, 0, nc.scalar if s < last - 1 else nc.gpsimd)
+                store(s, 0, whole if s < last - 2 else direct)
             if inside(s + 3):
                 turn_and_lace_x(s + 3)
 

@@ -158,12 +158,12 @@ def tile_sensor_residual_squared_d7_kernel(tc, x, g, a, w1_bytes, w1_scale, w2_b
                 in_=laced[w, c][:].rearrange("p n t -> p (n t)"),
             )
 
-        def sort_x(b, parts, copy):
+        def sort_x(b, parts, copy, run=2):
             if b not in x_sorted:
                 x_sorted[b] = work.tile([P, 4, 2, P], U32, name="x_sorted_tile", align_bytes=64, bufs=4)
             words = x_raw[b][:].rearrange("p r d -> p (r d)").bitcast(U32)
-            words = words.rearrange("p (c q i u) -> p c q u i", c=4, i=4, u=2)
-            target = x_sorted[b][:].rearrange("p c u (q i) -> p c q u i", i=4)
+            words = words.rearrange("p (c q i u) -> p c q u i", c=4, i=run, u=2)
+            target = x_sorted[b][:].rearrange("p c u (q i) -> p c q u i", i=run)
             copy(out=target[:, parts], in_=words[:, parts])
             for part in range(parts.start, parts.stop):
                 is_sorted.add((b, part))
@@ -415,14 +415,12 @@ def tile_sensor_residual_squared_d7_kernel(tc, x, g, a, w1_bytes, w1_scale, w2_b
             late = not inside(s + 3)
             lent = (2, 3) if late else (3,) if s > 0 else ()
             kept = [t for t in (2, 3) if t not in lent]
-            if s > 0:
-                product_direct(s - 1, 1)
             product_turned(s, both, (0, 1))
             if len(lent) == 1:
                 product_turned(s, both, (2,))
                 product_turned(s, both, (3,), turn_bank)
             else:
-                product_turned(s, both, (2, 3))
+                product_turned(s, both, (2, 3), turn_bank if late else mx_bank)
             first_product(s + 1, 0)
             if s > 0:
                 subtract_direct(s - 1, 1)
@@ -442,6 +440,7 @@ def tile_sensor_residual_squared_d7_kernel(tc, x, g, a, w1_bytes, w1_scale, w2_b
             product_direct(s, 0)
             for t in kept:
                 subtract_turned(s, both, t)
+            product_direct(s, 1)
             for r in range(2):
                 weigh(s + 1, r)
             subtract_direct(s, 0)
@@ -450,7 +449,7 @@ def tile_sensor_residual_squared_d7_kernel(tc, x, g, a, w1_bytes, w1_scale, w2_b
                 quantize_x(s + 2)
                 standardise(s + 2, h_home[s + 1][:])
             if inside(s + 5):
-                sort_x(s + 5, slice(0, 1), nc.gpsimd.tensor_copy)
+                sort_x(s + 5, slice(0, 1), nc.gpsimd.tensor_copy, run=4)
             for r in range(2):
                 open_back(s, r)
             for r in range(2):
@@ -464,8 +463,7 @@ def tile_sensor_residual_squared_d7_kernel(tc, x, g, a, w1_bytes, w1_scale, w2_b
             if inside(s + 3):
                 turn_and_lace_x(s + 3)
 
-        product_direct(14, 1)
-        product_turned(15, both, (2, 3))
+        product_turned(15, both, (2, 3), turn_bank)
         product_turned(15, both, (0, 1))
         product_direct(15, 0)
         subtract_direct(14, 1)

@@ -413,7 +413,7 @@ def tile_sensor_residual_squared_d7_kernel(tc, x, g, a, w1_bytes, w1_scale, w2_b
 
         for s in range(PAIRS - 1):
             late = not inside(s + 3)
-            lent = (2, 3) if late else (3,) if s > 0 else ()
+            lent = (2, 3) if late else (3,) if s % 4 > 0 else ()
             kept = [t for t in (2, 3) if t not in lent]
             product_turned(s, both, (0, 1))
             if len(lent) == 1:

@@ -397,6 +397,7 @@ def tile_sensor_residual_squared_d7_kernel(tc, x, g, a, w1_bytes, w1_scale, w2_b
         weigh(0, 0)
         lace_w2(TURNED, 0, nc.vector.tensor_copy)
         lace_w2(TURNED, 1, nc.scalar.copy)
+        sort_x(2, slice(2, 4), nc.scalar.copy)
         weigh(0, 1)
         for i in range(2):
             turn_w2(DIRECT, i, turn_bank)
@@ -408,10 +409,11 @@ def tile_sensor_residual_squared_d7_kernel(tc, x, g, a, w1_bytes, w1_scale, w2_b
         turn_and_lace_x(2)
         quantize_w(1, DIRECT)
         standardise(1, laced[1, DIRECT][:].rearrange("p (r n) t -> p r (n t)", r=2).bitcast(F32))
-        sort_x(3, slice(0, 2), nc.scalar.copy)
+        sort_x(3, slice(0, 4), nc.scalar.copy)
         make_g_diag((2, 3))
+        sort_x(4, slice(0, 2), nc.scalar.copy)
 
-        for s in range(PAIRS - 1):
+        for s in range(PAIRS - 2):
             late = not inside(s + 3)
             lent = (2, 3) if late else (3,) if s % 4 > 0 else ()
             kept = [t for t in (2, 3) if t not in lent]
@@ -434,9 +436,9 @@ def tile_sensor_residual_squared_d7_kernel(tc, x, g, a, w1_bytes, w1_scale, w2_b
             if s > 0:
                 if inside(s + 2):
                     square_direct(s - 1, 0)
-                    store(s - 1, 0, whole)
+                    store(s - 1, 0, whole if s < last - 2 else direct)
                 square_direct(s - 1, 1)
-                store(s - 1, 1, whole if s < last - 1 else direct)
+                store(s - 1, 1, whole if s < last - 2 else direct)
             product_direct(s, 0)
             for t in kept:
                 subtract_turned(s, both, t)
@@ -455,7 +457,7 @@ def tile_sensor_residual_squared_d7_kernel(tc, x, g, a, w1_bytes, w1_scale, w2_b
             for r in range(2):
                 turn_back(s, r)
                 square_turned(s, r)
-                if s >= last - 2:
+                if s >= last - 3:
                     store(s, r, turned)
             if not inside(s + 3):
                 square_direct(s, 0, nc.scalar if s < last - 1 else nc.gpsimd)
@@ -463,24 +465,53 @@ def tile_sensor_residual_squared_d7_kernel(tc, x, g, a, w1_bytes, w1_scale, w2_b
             if inside(s + 3):
                 turn_and_lace_x(s + 3)
 
+        product_turned(14, both, (0, 1))
+        product_turned(14, both, (2, 3), turn_bank)
+        first_product(15, 0)
+        subtract_direct(13, 1)
+        first_product(15, 1)
+        for t in (0, 1):
+            subtract_turned(14, both, t)
+        negate(14, both, (2, 3))
+        square_direct(13, 1)
+        store(13, 1, direct)
+        product_direct(14, 0)
+        weigh(15, 0)
+        product_direct(14, 1)
+        weigh(15, 1)
+        subtract_direct(14, 0)
+        quantize_h(15)
+        for r in both:
+            open_back(14, r)
+        for r in both:
+            turn_back(14, r)
+        subtract_direct(14, 1)
+        square_direct(14, 0, nc.gpsimd)
+        square_turned(14, 0)
+        store(14, 0, turned)
+        square_turned(14, 1)
+        store(14, 1, turned)
+        store(14, 0, direct)
+        product_direct(15, 0)
         product_turned(15, both, (2, 3), turn_bank)
         product_turned(15, both, (0, 1))
-        product_direct(15, 0)
-        subtract_direct(14, 1)
         product_direct(15, 1)
+        square_direct(14, 1, nc.scalar)
+        store(14, 1, direct)
+        subtract_direct(15, 0)
         negate(15, both, (2, 3))
         for t in (0, 1):
             subtract_turned(15, both, t)
-        square_direct(14, 1)
-        store(14, 1, direct)
-        for r in range(2):
+        for r in both:
             open_back(15, r)
-        for r in range(2):
-            subtract_direct(15, r)
-        for r in range(2):
+        subtract_direct(15, 1)
+        for r in both:
             turn_back(15, r)
-        for r in range(2):
-            square_direct(15, r, nc.vector)
-            square_turned(15, r)
-            store(15, r, turned)
-            store(15, r, direct)
+        square_direct(15, 0, nc.scalar)
+        store(15, 0, direct)
+        square_direct(15, 1, nc.vector)
+        store(15, 1, direct)
+        square_turned(15, 0)
+        store(15, 0, turned)
+        square_turned(15, 1)
+        store(15, 1, turned)

from contextlib import ExitStack

import concourse.mybir as mybir
from concourse.masks import make_identity

T, D, R = 4096, 1024, 512
FLOPS = 4 * T * D * R

F32 = mybir.dt.float32
BF16 = mybir.dt.bfloat16
U32 = mybir.dt.uint32
U8 = mybir.dt.uint8
E4M3 = mybir.dt.float8_e4m3fn
X4 = mybir.dt.float8_e4m3fn_x4
ALU = mybir.AluOpType
ACT = mybir.ActivationFunctionType

P = 128
HALF = 512
PAIRS = T // 256
TURNED, DIRECT = 0, 1
MX_BANKS, TURN_BANKS = 4, 4


def tile_sensor_residual_squared_d7_kernel(tc, x, g, a, w1_bytes, w1_scale, w2_bytes, w2_scale, out):
    nc = tc.nc
    x_pairs = x.rearrange("(b p r) d -> b p (r d)", p=P, r=2)
    out_pairs = out.rearrange("(b p r) d -> b p r d", p=P, r=2)

    with ExitStack() as ctx:
        keep = ctx.enter_context(tc.tile_pool(name="keep", bufs=1))
        work = ctx.enter_context(tc.tile_pool(name="work", bufs=3))
        psum = ctx.enter_context(tc.psum_pool(name="psum", bufs=1))
        ctx.enter_context(tc.manual_schedule())

        x_raw, x_sorted, x_quad, x_codes, x_scales = {}, {}, {}, {}, {}
        h_sums, h_home, h_codes, h_scales = {}, {}, {}, {}
        xg, y_turned, y_direct, e_turned, result, back_banks = {}, {}, {}, {}, {}, {}
        is_sorted = set()

        def inside(b):
            return 0 <= b < PAIRS

        def mx_bank(shape):
            return psum.tile(shape, F32, name="mx_bank", bufs=MX_BANKS)

        def turn_bank(shape):
            return psum.tile(shape, F32, name="turn_bank", bufs=TURN_BANKS)

        def row_tile(shape, dtype):
            return work.tile(shape, dtype, name="row_tile", align_bytes=64, bufs=8)

        def load_x(b):
            tile = keep.tile([P, 2, D], BF16, name="x_tile", align_bytes=64, bufs=PAIRS)
            nc.sync.dma_start(out=tile[:].rearrange("p r d -> p (r d)"), in_=x_pairs[b])
            x_raw[b] = tile

        w_raw = {(w, c): keep.tile([P, 4, R], U8, name="w_raw", align_bytes=64, bufs=4) for w in range(2) for c in range(2)}
        scale_cols = [keep.tile([P, 2, 4], F32, name="scale_cols", bufs=2) for w in range(2)]
        a_cols = keep.tile([P, 4], BF16, name="a_cols")
        g_cols = keep.tile([P, 4], BF16, name="g_cols")
        g_rows = keep.tile([P, HALF], BF16, name="g_rows", align_bytes=64)

        def load_w(w, c):
            rows = (w1_bytes, w2_bytes)[w].rearrange("(c p t) n -> c p (t n)", p=P, t=4)
            nc.sync.dma_start(out=w_raw[w, c][:].rearrange("p t n -> p (t n)"), in_=rows[c])

        def load_scales(queue, w):
            block_rows = (w1_scale, w2_scale)[w].rearrange("(c q) j -> q c j", q=4)
            for q in range(4):
                queue.dma_start(out=scale_cols[w][32 * q : 32 * q + 32], in_=block_rows[q].partition_broadcast(32))

        def load_a(queue):
            queue.dma_start(out=a_cols[:], in_=a.rearrange("(p t) -> p t", t=4))

        def load_g_rows(queue):
            queue.dma_start(out=g_rows[:], in_=g[HALF:].partition_broadcast(P))

        def load_g_cols(queue):
            queue.dma_start(out=g_cols[:], in_=g[0:HALF].rearrange("(p t) -> p t", t=4))

        load_scales(nc.scalar, 0)
        for c in range(2):
            load_w(0, c)
        for b in range(2):
            load_x(b)
        load_scales(nc.sync, 1)
        for c in range(2):
            load_w(1, c)
        load_a(nc.sync)
        load_g_rows(nc.sync)
        for b in range(2, 4):
            load_x(b)
        load_g_cols(nc.sync)
        for b in range(4, PAIRS):
            load_x(b)

        ident = keep.tile([P, P], F32, name="ident", align_bytes=64)
        make_identity(nc, ident[:])

        w1_wide = [row_tile([P, 4, R], BF16) for c in range(2)]
        laced = {(0, c): row_tile([P, R, 4], BF16) for c in range(2)}
        w2_scaled = [row_tile([P, 4, R], BF16) for c in range(2)]
        for c in range(2):
            laced[1, c] = row_tile([P, R, 4], BF16)
        w_codes = [keep.tile([P, 2, R], U32, name="w_codes", align_bytes=64, bufs=2) for w in range(2)]
        w_scales = [keep.tile([P, 2, R], U8, name="w_scales", align_bytes=64, bufs=2) for w in range(2)]
        w2_banks = {}

        def widen_w1():
            raw = [w_raw[0, c][:].rearrange("p t n -> p (t n)").bitcast(E4M3) for c in range(2)]
            wide = [w1_wide[c][:].rearrange("p t n -> p (t n)") for c in range(2)]
            nc.vector.tensor_copy(out=wide[0], in_=raw[0])
            nc.scalar.activation(out=wide[1][:, 0:P], in_=raw[1][:, 0:P], func=ACT.Copy)
            nc.scalar.copy(out=wide[1][:, P:], in_=raw[1][:, P:])

        def lace_w1(c, j, on_scalar):
            out_ = laced[0, c][:].rearrange("p (u m) t -> p m u t", u=4)[:, 32 * j : 32 * j + 32]
            in_ = w1_wide[c][:, :, 128 * j : 128 * j + 128].rearrange("p t (m u) -> p m u t", u=4)
            scale = scale_cols[0][:, c, j : j + 1]
            if on_scalar:
                nc.scalar.activation(out=out_, in_=in_, func=ACT.Copy, scale=scale)
            else:
                nc.vector.tensor_scalar(out=out_, in0=in_, scalar1=scale, scalar2=None, op0=ALU.mult)

        def scale_w2(c, rows, on_scalar):
            for t in rows:
                for j in range(4):
                    columns = slice(128 * j, 128 * j + 128)
                    out_, in_ = w2_scaled[c][:, t, columns], w_raw[1, c][:, t, columns].bitcast(E4M3)
                    scale = scale_cols[1][:, c, j : j + 1]
                    if on_scalar:
                        nc.scalar.activation(out=out_, in_=in_, func=ACT.Copy, scale=scale)
                    else:
                        nc.vector.tensor_scalar(out=out_, in0=in_, scalar1=scale, scalar2=None, op0=ALU.mult)

        def turn_w2(c, i, new_bank):
            bank = new_bank([P, 2, 2, P])
            for k in range(2):
                words = w2_scaled[c][:, 2 * i + k, :].bitcast(F32)
                for u in range(2):
                    nc.tensor.transpose(bank[:, k, u, :], words[:, u::2], ident[:])
            w2_banks[c, i] = bank

        def lace_w2(c, i, copy):
            words, bank = laced[1, c][:].bitcast(F32), w2_banks[c, i]
            if c == TURNED:
                out_ = words.rearrange("p (t m) u -> p t m u", t=4)[:, 2 * i : 2 * i + 2]
                copy(out=out_, in_=bank[:].rearrange("p k u m -> p k m u"))
            else:
                out_ = words.rearrange("p (m t) u -> p m t u", t=4)[:, :, 2 * i : 2 * i + 2, :]
                copy(out=out_, in_=bank[:].rearrange("p k u m -> p m k u"))

        def quantize_w(w, c):
            nc.vector.quantize_mx(
                out=w_codes[w][:, c, :].bitcast(X4),
                scales=w_scales[w][:, c, :],
                in_=laced[w, c][:].rearrange("p n t -> p (n t)"),
            )

        def sort_x(b, parts, copy, run=2):
            if b not in x_sorted:
                x_sorted[b] = work.tile([P, 4, 2, P], U32, name="x_sorted_tile", align_bytes=64, bufs=4)
            words = x_raw[b][:].rearrange("p r d -> p (r d)").bitcast(U32)
            words = words.rearrange("p (c q i u) -> p c q u i", c=4, i=run, u=2)
            target = x_sorted[b][:].rearrange("p c u (q i) -> p c q u i", i=run)
            copy(out=target[:, parts], in_=words[:, parts])
            for part in range(parts.start, parts.stop):
                is_sorted.add((b, part))

        def turn_x(b, r, new_bank):
            bank = new_bank([P, 2, 2, P])
            words = x_raw[b][:, r, :].bitcast(F32)
            for c in range(2):
                for u in range(2):
                    if (b, 2 * r + c) in is_sorted:
                        source = x_sorted[b][:, 2 * r + c, u, :].bitcast(F32)
                    else:
                        source = words[:, 256 * c + u : 256 * (c + 1) : 2]
                    nc.tensor.transpose(bank[:, c, u, :], source, ident[:])
            return bank

        def x_laced(b):
            return x_quad[b // 2][:, b % 2]

        def lace_x(b, r, bank, copy):
            if b // 2 not in x_quad:
                x_quad[b // 2] = work.tile([P, 2, 2, 256, 4], BF16, name="x_quad_tile", align_bytes=64, bufs=3)
            copy(
                out=x_laced(b)[:, :, 128 * r : 128 * r + 128, :].bitcast(F32).rearrange("p c (n e) u -> p c n u e", e=2),
                in_=bank[:].rearrange("p c u (n e) -> p c n u e", e=2),
            )

        def turn_and_lace_x(b):
            for r in range(2):
                lace_x(b, r, turn_x(b, r, turn_bank), nc.scalar.copy)

        def quantize_x(b):
            x_codes[b] = work.tile([P, 2, 256], U32, name="x_codes_tile", align_bytes=64)
            x_scales[b] = work.tile([P, 2, 256], U8, name="x_scales_tile", align_bytes=64)
            nc.vector.quantize_mx(
                out=x_codes[b][:].rearrange("p c n -> p (c n)").bitcast(X4),
                scales=x_scales[b][:].rearrange("p c n -> p (c n)"),
                in_=x_laced(b).rearrange("p c n t -> p (c n t)"),
            )

        def first_product(b, r):
            bank = mx_bank([P, 4, P])
            tokens = slice(128 * r, 128 * r + 128)
            for u in range(4):
                columns = slice(128 * u, 128 * u + 128)
                for c in range(2):
                    nc.tensor.matmul_mx(
                        out=bank[:, u, :],
                        lhsT=w_codes[0][:, c, columns].bitcast(X4),
                        lhsT_scale=w_scales[0][:, c, columns],
                        rhs=x_codes[b][:, c, tokens].bitcast(X4),
                        rhs_scale=x_scales[b][:, c, tokens],
                        start=(c == 0),
                        stop=(c == 1),
                    )
            h_sums[b, r] = bank

        def h_values(b):
            return h_home[b][:, 0, :].bitcast(BF16)

        def weigh(b, r):
            if r == 0:
                h_home[b] = work.tile([P, 2, HALF], F32, name="h_home_tile", align_bytes=64, bufs=5)
            nc.vector.tensor_tensor(
                out=h_values(b)[:, HALF * r : HALF * (r + 1)].rearrange("p (n e u) -> p n u e", e=2, u=4),
                in0=h_sums[b, r][:].rearrange("p u (n e) -> p n u e", e=2),
                in1=a_cols[:].unsqueeze(1).unsqueeze(3).to_broadcast([P, P // 2, 4, 2]),
                op=ALU.mult,
            )

        def quantize_h(b, tiles=(0, 1)):
            if b // 2 not in h_codes:
                h_codes[b // 2] = work.tile([P, HALF], U32, name="h_codes_tile", align_bytes=64)
                h_scales[b // 2] = work.tile([P, HALF], U8, name="h_scales_tile", align_bytes=64)
            tokens = tokens_of(b, tiles)
            nc.vector.quantize_mx(
                out=h_codes[b // 2][:, tokens].bitcast(X4),
                scales=h_scales[b // 2][:, tokens],
                in_=h_values(b)[:, HALF * tiles[0] : HALF * (tiles[-1] + 1)],
            )

        def standardise(b, home, tiles=slice(0, 2), engine=nc.gpsimd):
            for r in range(tiles.start, tiles.stop):
                xg[b, r] = home[:, r - tiles.start, :]
            engine.tensor_tensor(
                out=home,
                in0=x_raw[b][:, tiles, HALF:],
                in1=g_rows[:].unsqueeze(1).to_broadcast([P, tiles.stop - tiles.start, HALF]),
                op=ALU.mult,
            )

        def result_of(b, r):
            if (b, r) not in result:
                result[b, r] = row_tile([P, D], F32)
            return result[b, r]

        on_tensor = set()
        g_wide = keep.tile([P, 4], F32, name="g_wide")
        g_diag = keep.tile([P, 4, P], BF16, name="g_diag", align_bytes=64)

        def make_g_diag(planes):
            nc.scalar.activation(out=g_wide[:], in_=g_cols[:], func=ACT.Copy)
            for t in planes:
                nc.scalar.activation(out=g_diag[:, t, :], in_=ident[:], func=ACT.Copy, scale=g_wide[:, t : t + 1])

        def tokens_of(b, tiles):
            return slice(256 * (b % 2) + 128 * tiles[0], 256 * (b % 2) + 128 * (tiles[-1] + 1))

        def product_turned(b, tiles, planes, new_bank=mx_bank):
            bank = new_bank([P, len(planes), 128 * len(tiles)])
            tokens = tokens_of(b, tiles)
            for k, t in enumerate(planes):
                columns = slice(128 * t, 128 * t + 128)
                nc.tensor.matmul_mx(
                    out=bank[:, k, :],
                    lhsT=w_codes[1][:, TURNED, columns].bitcast(X4),
                    lhsT_scale=w_scales[1][:, TURNED, columns],
                    rhs=h_codes[b // 2][:, tokens].bitcast(X4),
                    rhs_scale=h_scales[b // 2][:, tokens],
                    start=True,
                    stop=True,
                )
                y_turned[b, tiles, t] = (bank, k)

        def e_planes(b, tiles):
            if b // 2 not in e_turned:
                e_turned[b // 2] = work.tile([P, 4, HALF], F32, name="e_turned_tile", align_bytes=64, bufs=2)
            return e_turned[b // 2][:, :, tokens_of(b, tiles)]

        def subtract_turned(b, tiles, t):
            bank, k = y_turned[b, tiles, t]
            nc.vector.scalar_tensor_tensor(
                out=e_planes(b, tiles)[:, t, :],
                in0=x_laced(b)[:, TURNED, 128 * tiles[0] : 128 * (tiles[-1] + 1), t],
                scalar=g_cols[:, t : t + 1],
                in1=bank[:, k, :],
                op0=ALU.mult,
                op1=ALU.subtract,
            )

        def negate(b, tiles, planes):
            bank, k = y_turned[b, tiles, planes[0]]
            for r in tiles:
                for t in planes:
                    on_tensor.add((b, r, t))
            nc.scalar.activation(
                out=e_planes(b, tiles)[:, planes[0] : planes[-1] + 1, :],
                in_=bank[:, k : k + len(planes), :],
                func=ACT.Copy,
                scale=-1.0,
            )

        def open_back(b, r, new_bank=turn_bank):
            back_banks[b, r] = new_bank([P, 4, P])
            planes = [t for t in range(4) if (b, r, t) in on_tensor]
            for t in planes:
                x_plane = x_laced(b)[:, TURNED, 128 * r : 128 * r + 128, t]
                nc.tensor.matmul(back_banks[b, r][:, t, :], x_plane, g_diag[:, t, :], start=(t == planes[0]), stop=False)

        def turn_back(b, r):
            bank = back_banks[b, r]
            planes = [t for t in range(4) if (b, r, t) in on_tensor]
            first = 256 * (b % 2) + 128 * r
            for t in planes + [t for t in range(4) if t not in planes]:
                source = e_turned[b // 2][:, t, first : first + 128]
                if t in planes:
                    nc.tensor.matmul(bank[:, t, :], source, ident[:], start=False, stop=(t == planes[-1]), is_transpose=True)
                else:
                    nc.tensor.transpose(bank[:, t, :], source, ident[:])

        def square_turned(b, r):
            nc.scalar.activation(
                out=result_of(b, r)[:, 0:HALF].rearrange("p (m t) -> p m t", t=4),
                in_=back_banks[b, r][:].rearrange("p t m -> p m t"),
                func=ACT.Square,
            )

        def product_direct(b, r):
            first = 256 * (b % 2) + 128 * r
            tokens = slice(first, first + 128)
            bank = mx_bank([P, HALF])
            nc.tensor.matmul_mx(
                out=bank[:],
                lhsT=h_codes[b // 2][:, tokens].bitcast(X4),
                lhsT_scale=h_scales[b // 2][:, tokens],
                rhs=w_codes[1][:, DIRECT, :].bitcast(X4),
                rhs_scale=w_scales[1][:, DIRECT, :],
                start=True,
                stop=True,
            )
            y_direct[b, r] = bank

        def subtract_direct(b, r, columns=slice(0, HALF)):
            tile = xg[b, r][:, columns]
            nc.vector.tensor_tensor(out=tile, in0=tile, in1=y_direct[b, r][:, columns], op=ALU.subtract)

        def square_direct(b, r, engine=nc.scalar, columns=slice(0, HALF)):
            tile, target = xg[b, r][:, columns], result_of(b, r)[:, HALF:][:, columns]
            if engine is nc.scalar:
                nc.scalar.activation(out=target, in_=tile, func=ACT.Square)
            else:
                engine.tensor_tensor(out=target, in0=tile, in1=tile, op=ALU.mult)

        def store(b, r, sensors):
            nc.sync.dma_start(out=out_pairs[b][:, r, sensors], in_=result[b, r][:, sensors])

        both = (0, 1)
        whole, turned, direct, last = slice(0, D), slice(0, HALF), slice(HALF, D), PAIRS - 1

        widen_w1()
        for j in (2, 3):
            lace_w1(1, j, on_scalar=True)
        banks = [(b, r, turn_x(b, r, turn_bank)) for b in range(2) for r in range(2)]
        for j in range(4):
            lace_w1(0, j, on_scalar=False)
        for j in (0, 1):
            lace_w1(1, j, on_scalar=False)
        for args in banks:
            lace_x(*args, nc.scalar.copy)
        for c in range(2):
            quantize_w(0, c)
        quantize_x(0)
        scale_w2(TURNED, range(4), on_scalar=False)
        scale_w2(DIRECT, range(4), on_scalar=True)
        first_product(0, 0)
        for i in range(2):
            turn_w2(TURNED, i, turn_bank)
        first_product(0, 1)
        quantize_x(1)
        standardise(0, x_quad[0][:, 1:2, DIRECT].rearrange("p b n t -> p b (n t)").bitcast(F32), slice(1, 2))
        weigh(0, 0)
        lace_w2(TURNED, 0, nc.vector.tensor_copy)
        lace_w2(TURNED, 1, nc.scalar.copy)
        sort_x(2, slice(2, 4), nc.scalar.copy)
        weigh(0, 1)
        for i in range(2):
            turn_w2(DIRECT, i, turn_bank)
        quantize_w(1, TURNED)
        quantize_h(0)
        standardise(0, x_quad[0][:, 0:1, DIRECT].rearrange("p b n t -> p b (n t)").bitcast(F32), slice(0, 1), nc.vector)
        for i in range(2):
            lace_w2(DIRECT, i, nc.scalar.copy)
        turn_and_lace_x(2)
        quantize_w(1, DIRECT)
        standardise(1, laced[1, DIRECT][:].rearrange("p (r n) t -> p r (n t)", r=2).bitcast(F32))
        sort_x(3, slice(0, 4), nc.scalar.copy)
        make_g_diag((2, 3))
        sort_x(4, slice(0, 2), nc.scalar.copy)

        for s in range(PAIRS - 2):
            late = not inside(s + 3)
            lent = (2, 3) if late else (3,) if s % 4 > 0 else ()
            kept = [t for t in (2, 3) if t not in lent]
            product_turned(s, both, (0, 1))
            if len(lent) == 1:
                product_turned(s, both, (2,))
                product_turned(s, both, (3,), turn_bank)
            else:
                product_turned(s, both, (2, 3), turn_bank if late else mx_bank)
            first_product(s + 1, 0)
            if s > 0:
                subtract_direct(s - 1, 1)
            first_product(s + 1, 1)
            for t in (0, 1):
                subtract_turned(s, both, t)
            if lent:
                negate(s, both, lent)
            if s > 0 and inside(s + 3):
                sort_x(s + 3, slice(2, 4), nc.scalar.copy)
            if s > 0:
                if inside(s + 2):
                    square_direct(s - 1, 0)
                    store(s - 1, 0, whole if s < last - 2 else direct)
                square_direct(s - 1, 1)
                store(s - 1, 1, whole if s < last - 2 else direct)
            product_direct(s, 0)
            for t in kept:
                subtract_turned(s, both, t)
            product_direct(s, 1)
            for r in range(2):
                weigh(s + 1, r)
            subtract_direct(s, 0)
            quantize_h(s + 1)
            if inside(s + 2):
                quantize_x(s + 2)
                standardise(s + 2, h_home[s + 1][:])
            if inside(s + 5):
                sort_x(s + 5, slice(0, 1), nc.gpsimd.tensor_copy, run=4)
            for r in range(2):
                open_back(s, r)
            for r in range(2):
                turn_back(s, r)
                square_turned(s, r)
                if s >= last - 3:
                    store(s, r, turned)
            if not inside(s + 3):
                square_direct(s, 0, nc.scalar if s < last - 1 else nc.gpsimd)
                store(s, 0, whole if s < last - 2 else direct)
            if inside(s + 3):
                turn_and_lace_x(s + 3)

        product_turned(14, both, (0, 1))
        product_turned(14, both, (2, 3), turn_bank)
        first_product(15, 0)
        subtract_direct(13, 1)
        first_product(15, 1)
        for t in (0, 1):
            subtract_turned(14, both, t)
        negate(14, both, (2, 3))
        square_direct(13, 1)
        store(13, 1, direct)
        product_direct(14, 0)
        weigh(15, 0)
        product_direct(14, 1)
        weigh(15, 1)
        subtract_direct(14, 0)
        quantize_h(15)
        for r in both:
            open_back(14, r)
        for r in both:
            turn_back(14, r)
        subtract_direct(14, 1)
        square_direct(14, 0, nc.gpsimd)
        square_turned(14, 0)
        store(14, 0, turned)
        square_turned(14, 1)
        store(14, 1, turned)
        store(14, 0, direct)
        product_direct(15, 0)
        product_turned(15, both, (2, 3), turn_bank)
        product_turned(15, both, (0, 1))
        product_direct(15, 1)
        square_direct(14, 1, nc.scalar)
        store(14, 1, direct)
        subtract_direct(15, 0)
        negate(15, both, (2, 3))
        for t in (0, 1):
            subtract_turned(15, both, t)
        for r in both:
            open_back(15, r)
        subtract_direct(15, 1)
        for r in both:
            turn_back(15, r)
        square_direct(15, 0, nc.scalar)
        store(15, 0, direct)
        square_direct(15, 1, nc.vector)
        store(15, 1, direct)
        square_turned(15, 0)
        store(15, 0, turned)
        square_turned(15, 1)
        store(15, 1, turned)
